import numpy as np, ml_dtypes
CORES = [83,85,87,115,117,119]
N = 6
BF = ml_dtypes.bfloat16
W, SV, M, HOPS = 4096, 512, 192, [1, 2, 3]
RO = len(HOPS) + 1
def names(rng, power, *shape):
    return np.minimum((W * rng.random(shape) ** power).astype(np.int64), W - 1)
def pairs(rng, C, power):
    a = names(rng, power, N, 8, 16, C); b = np.take_along_axis(a, np.argsort(rng.random((N, 8, 16, C)), axis=2), 2)
    share = rng.choice(np.array([0.0, 0.15, 0.5, 1.0]), (N, 8, 1, C)); b = np.where(rng.random(b.shape) < share, b, names(rng, power, N, 8, 16, C))
    fa = rng.choice(np.array([0.05, 0.12, 0.3, 0.7, 1.0]), (N, 8, 1, C), p=[0.2, 0.25, 0.2, 0.2, 0.15])
    fb = rng.choice(np.array([0.0, 0.3, 0.7, 1.0]), (N, 8, 1, C), p=[0.05, 0.25, 0.3, 0.4])
    return np.where(rng.random(a.shape) < fa, a, -1), np.where(rng.random(b.shape) < fb, b, -1)
def parts(rng, power):
    clk = rng.integers(0, 256, (N, 8, 16, W)); z = rng.integers(0, 256, (N, 8, 16, M)); th = rng.integers(1200, 1600, (N, 8))
    sc, st = pairs(rng, SV, power); d, t = pairs(rng, M, power)
    return clk, sc, st, d, t, z, th
def pack(clk, sc, st, d, t, z, th):
    return {"clk": clk.reshape(N, 128, W).astype(np.float32).astype(BF), "sc": sc.reshape(N, 128, SV).astype(np.int32), "st": st.reshape(N, 128, SV).astype(np.int32),
            "dl": d.reshape(N, 128, M).astype(np.int32), "tl": t.reshape(N, 128, M).astype(np.int32), "z0": z.reshape(N, 128, M).astype(np.float32).astype(BF),
            "th": np.repeat(th.reshape(N, 8), 16, axis=1).reshape(N, 128, 1).astype(np.int32)}
def setup_inputs(rng):
    return pack(*parts(rng, 1))
def setup_inputs_spread(rng):
    clk, sc, st, d, t, z, th = parts(rng, 4)
    clk = np.floor(np.exp2(8 * rng.random((N, 8, 1, W))) * rng.random((N, 8, 16, W))).astype(np.int64)
    z = np.floor(np.exp2(8 * rng.random((N, 8, 1, M))) * rng.random((N, 8, 16, M))).astype(np.int64)
    th = np.minimum(np.floor(np.exp2(12 * rng.random((N, 8)))).astype(np.int64), 4080)
    return pack(np.minimum(clk, 255), sc, st, d, t, np.minimum(z, 255), th)
def setup_inputs_ends(rng):
    def rec(C):
        p = rng.choice(np.array([0.0, 0.06, 0.5, 1.0]), (N, 8, 1, C)); s = (N, 8, 16, C)
        a = np.where(rng.random(s) < p, W - 1, -1)
        o = np.where(rng.random(s) < 0.3, -1, np.where(rng.random(s) < 0.15, W - 1, rng.integers(0, W, s)))
        return np.where(rng.random((N, 8, 1, C)) < 0.6, a, o)
    def half(C):
        k = rng.integers(0, 3, (N, 8, 1, C))
        return np.where(k == 0, 0, np.where(k == 1, 255, 255 * rng.integers(0, 2, (N, 8, 16, C))))
    clk = half(W); z = half(M); sc = rec(SV); st = rec(SV); d = rec(M); t = rec(M)
    g = np.arange(8)[None, :]; q = np.arange(N)[:, None]
    clk[..., 0] = 255; clk[..., W - 1] = np.where(((g + q + N) & 1) == 0, 255, 0)[:, :, None]
    clk[..., W - 2] = 255; clk[:, :, 15, W - 2] = 254
    z[..., 0] = 255; z[..., M - 1] = 255; z[..., M - 2] = 0
    th = 4080 * ((g // 2 + q + rng.integers(0, 2, (N, 1))) & 1); th[:, 5] = 4080
    for m, lo, hi in ((M - 1, 0, W - 1), (0, W - 1, 0)):
        d[..., m] = -1; d[:, :, 15, m] = W - 1; d[:, :, 4, m] = 5; t[..., m] = -1; t[:, :, 2, m] = lo; t[:, :, 15, m] = hi
    s = slice(M - 6, M - 2); z[..., s] = 255; d[:, :, 15, s] = W - 1; t[..., s] = -1; t[:, :, 2, s] = W - 2; t[:, :, 15, s] = 0
    d[:, 5] = W - 1; t[:, 5] = W - 1; sc[:, 5] = W - 1; st[:, 5] = W - 1; z[:, 5] = z[:, 5, :1]
    return pack(clk, sc, st, d, t, z, th)
def setup_inputs_corners(rng):
    clk, sc, st, d, t, z, th = parts(rng, 1)
    clk[:, 1::2, :, 1::2] = clk[:, 1::2, :, 0::2]
    th = rng.choice(np.array([0, 1, 126, 128, 1000, 1999, 4080]), (N, 8)); th[:, 0] = 1000; th[:, 7] = 1999; th[:, 3] = 0
    th[:, 5] = 2051 + 4 * rng.integers(0, 100, N); th[:, 6] = 2052 + 4 * rng.integers(0, 100, N)
    lanes = np.array([0, 1, SV - 1, SV, W - 2, W - 1])
    for q in range(N):
        for g in range(8):
            kind = rng.permutation(M) % 10; n = np.where(rng.random(M) < 0.5, rng.choice(lanes, M), rng.integers(0, W, M)); full = rng.integers(0, W, (16, M))
            D = d[q, g]; T = t[q, g]; x = clk[q, g][:, n]; room = np.maximum(x, 255 - x)
            gap = np.maximum(int(th[q, g]) + rng.integers(-1, 2, M), 0); step = np.clip(gap[None, :] - (np.add.accumulate(room, axis=0) - room), 0, room)
            near = np.where(x < 128, x + step, x - step)
            s = kind == 0; D[:, s] = -1; T[:, s] = -1; T[15, s] = n[s]
            s = kind == 1; D[:, s] = -1; T[:, s] = -1
            s = kind == 2; D[:, s] = full[:, s]; T[:, s] = -1
            s = kind == 3; D[:, s] = full[:, s]; T[:, s] = full[::-1][:, s]
            s = kind == 4; D[:, s] = n[s]; T[:, s] = -1; T[15, s] = n[s]
            s = kind == 5; D[:, s] = full[:, s] & ~1; T[:, s] = full[::-1][:, s] | 1
            s = kind == 6; D[:, s] = -1; D[15, s] = n[s]; T[:, s] = -1; T[0, s] = n[s]
            s = kind == 7; D[:, s] = -1; D[0, s] = n[s]; T[:, s] = -1; T[15, s] = n[s] ^ 1
            s = kind == 8; D[:, s] = -1; D[7, s] = n[s]; D[8, s] = (n[s] + 5) % W; T[:, s] = -1; T[15, s] = n[s]; T[3, s] = n[s] ^ 1
            s = kind == 9; D[:, s] = n[s]; D[0, s] = n[s] ^ 1; T[:, s] = n[s]
            s = (kind == 4) | (kind == 6) | (kind == 8) | (kind == 9); z[q, g][:, s] = near[:, s]
    k = rng.integers(0, 6, (N, 8, 1, SV)); more = rng.integers(0, W, (2, N, 8, 16, SV))
    st = np.where(k == 4, sc[:, :, ::-1], st)
    sc = np.where((k == 0) | (k == 2), -1, np.where(k == 1, more[0], sc)); st = np.where((k == 0) | (k == 3), -1, np.where(k == 1, more[1], st))
    return pack(clk, sc, st, d, t, z, th)
def setup_inputs_crowd(rng):
    clk, sc, st, d, t, z, th = parts(rng, 1); h = SV >> 1
    def high(*shape):
        return h + rng.integers(0, h - 1, shape) + SV * rng.integers(0, W // SV, shape)
    for q in range(N):
        for g in (0, 1):
            keep = d[q, g, :, M - 1].copy(), z[q, g, :, M - 1].copy()
            z[q, g] = rng.permuted(np.repeat(rng.integers(0, 256, (16, 1)), M, axis=1), axis=0); t[q, g] = -1
            if g == 1: d[q, g, :, M - 1], z[q, g, :, M - 1] = keep; t[q, g, 15, M - 1] = W - 1
        for g in (2, 3):
            v = int(rng.choice(np.array([0, SV - 1, SV >> 1]))); n = v + SV * rng.integers(0, W // SV, (16, M))
            t[q, g] = np.where(rng.random((16, M)) < 0.5, n, -1); t[q, g, 9] = n[9]; d[q, g] = -1
            if g == 3: d[q, g, 15, M - 1] = (v + 1) % W
        for g in (6, 7):
            n = rng.integers(0, W, M); z[q, g] = clk[q, g][:, n]; t[q, g, 5] = n
            d[q, g] = -1; d[q, g, 15] = n
            if g == 7: d[q, g, 15, M - 1] = -1
    for g, c, lim in ((4, 20, 219), (5, 35, 212)):
        clk[:, g] = rng.integers(0, 8, (N, 16, W)); clk[:, g, :, W - 1] = c
        d[:, g] = high(N, 16, M); t[:, g] = rng.permuted(d[:, g], axis=1)
        sc[:, g, :, :h] = high(N, 16, h); st[:, g, :, :h] = rng.permuted(sc[:, g, :, :h], axis=1)
        z[:, g] = rng.integers(0, 7, (N, 16, M))
        for q in range(N):
            z[q, g, :, M - 1] = 6 + (np.arange(16) < 4 + q)
            b = (q + int(np.sum(HOPS[:-1]))) % N; sc[b, g, :, 100 + q] = W - 1; st[b, g, :, 100 + q] = W - 1
            th[(b + HOPS[-1]) % N, g] = lim - q
    d[:, 5, 15, 0] = -1
    return pack(clk, sc, st, d, t, z, th)
def check_inputs(d):
    bad = []
    for k, lo, hi in (("clk", 0, 255), ("z0", 0, 255), ("sc", -1, W - 1), ("st", -1, W - 1), ("dl", -1, W - 1), ("tl", -1, W - 1), ("th", 0, 4080)):
        a = np.asarray(d[k]).astype(np.float64)
        if not (np.min(a) >= lo and np.max(a) <= hi): bad.append("range of " + k)
        elif np.any(a != np.floor(a)): bad.append("whole numbers in " + k)
    h = np.asarray(d["th"]).reshape(-1, 16)
    if np.any(h != h[:, :1]): bad.append("th alike in a group")
    return bad
def reference(clk, sc, st, dl, tl, z0, th):
    X = clk.astype(np.float32).astype(np.int64).reshape(N, 8, 16, W); Z = z0.astype(np.float32).astype(np.int64).reshape(N, 8, 16, M)
    C = sc.astype(np.int64).reshape(N, 8, 16, SV); S = st.astype(np.int64).reshape(N, 8, 16, SV)
    D = dl.astype(np.int64).reshape(N, 8, 16, M); T = tl.astype(np.int64).reshape(N, 8, 16, M)
    base = th.astype(np.int64).reshape(N, 8, 16)[:, :, 0]; A = np.zeros((N, 8), np.int64); row = np.arange(16).reshape(1, 16, 1)
    for visit in range(RO):
        nd, nt, nz = [], [], []
        for a in range(N):
            d, t, z = D[a], T[a], Z[a]
            x = np.take_along_axis(X[a], np.maximum(d, 0).reshape(8, 1, 16 * M), 2).reshape(8, 16, 16, M)
            y = np.take_along_axis(X[a], np.maximum(t, 0).reshape(8, 1, 16 * M), 2).reshape(8, 16, 16, M)
            dist = np.sum(np.abs(x - z[:, :, None, :]), axis=1)
            score = np.where(t >= 0, np.sum(np.minimum(y, z[:, :, None, :]), axis=1), -1)
            ks = np.argmax(score, axis=1)
            has = np.any(t >= 0, axis=1); v = np.take_along_axis(t, ks[:, None, :], 1)[:, 0] & (SV - 1)
            eq = (d[:, :, None, :] == t[:, None, :, :]) & (d >= 0)[:, :, None, :]
            cd = np.any(eq, axis=2); ct = np.any(eq, axis=1)
            lim = base[a] + 8 * (A[a] & 31)
            abort = np.any(cd & (dist > lim[:, None, None]), axis=1)
            d1 = np.where(cd, -1, d); t1 = np.where(ct | (row == ks[:, None, :]), -1, t)
            left = np.any(d1 >= 0, axis=1); proof = has & ~abort & ~left; go = has & ~abort & left
            yk = np.take_along_axis(y, ks[:, None, None, :], 2)[:, :, 0]
            top = np.max(np.where((d1 >= 0)[:, None, :, :], x, 0), axis=2)
            cv = np.take_along_axis(C[a], v[:, None, :], 2); sv = np.take_along_axis(S[a], v[:, None, :], 2)
            u = np.sum(z, axis=1) & (SV - 1)
            cu = np.take_along_axis(C[a], u[:, None, :], 2); su = np.take_along_axis(S[a], u[:, None, :], 2)
            hd = np.any(cv[:, :, None, :] == d[:, None, :, :], axis=2); ht = np.any(sv[:, :, None, :] == t[:, None, :, :], axis=2)
            d2 = np.where((d1 < 0) & ~hd, cv, d1); t2 = np.where((t1 < 0) & ~ht, sv, t1)
            ab = abort[:, None, :]; on = go[:, None, :]
            nd.append(np.where(ab, cv, np.where(on, d2, cu))); nt.append(np.where(ab, sv, np.where(on, t2, su)))
            nz.append(np.where(ab, np.abs(z - yk), np.where(on, (yk + top) >> 1, z)))
            A[a] += np.sum(cd & ~ab, axis=(1, 2))
            for g in range(8):
                for m in np.nonzero(proof[g])[0]: C[a, g, :, v[g, m]] = t1[g, :, m]
        D, T, Z = np.stack(nd), np.stack(nt), np.stack(nz)
        if visit < RO - 1: D, T, Z = [np.roll(b, HOPS[visit], axis=0) for b in (D, T, Z)]
    return {"yd": D.reshape(N, 128, M).astype(np.float32), "yt": T.reshape(N, 128, M).astype(np.float32), "yz": Z.reshape(N, 128, M).astype(np.float32), "ys": C.reshape(N, 128, SV).astype(np.float32)}

@@ -1,0 +1,505 @@
+import numpy as np
+from concourse.mybir import dt, AluOpType as A, ActivationFunctionType as F
+
+N = 6
+HOPS = [1, 2, 3]
+M, C, NC = 192, 96, 6
+L = 16 * C
+BIG = 30000.0
+
+H, BF, F4, I4, U2 = "float16", "bfloat16", "float32", "int32", "uint16"
+PER = {
+    "OFF": (U2, 192), "OFX": (U2, 96), "OFN": (U2, 8), "LI": (I4, 192), "KI": (I4, 8),
+    "ZSS": (BF, L), "ZE": (H, L), "MT": (H, L), "SD": (H, L), "AD": (H, L), "XT": (H, L), "TP": (H, L),
+    "EQ0": (H, L), "EQ1": (H, L), "EQ2": (H, L), "CX": (H, 3 * L),
+    "FL": (H, 192), "QL": (H, 8), "OH": (H, 96), "TH": (H, 96), "NH": (H, 96),
+    "CS": (H, 192), "CT": (H, 192), "YK": (H, 96), "F1": (H, 96), "FAR": (H, 96),
+    "DT1": (H, 192), "FD1": (H, 192), "HC": (H, 192), "P1": (H, 192), "P2": (H, 192), "P3": (H, 192),
+    "ZA": (H, 96), "ZA2": (H, 96), "ZG": (H, 96), "ZGI": (H, 96), "ZG2": (H, 96), "ZR": (H, 96),
+    "FIN": (H, 288), "FSG": (H, 192), "FNE": (H, 192), "TSG": (H, 96), "TNE": (H, 96),
+    "MX": (F4, 96), "JK": (F4, 96), "T1": (F4, 192), "OUT": (F4, 288), "TD": (F4, 96),
+}
+ONE = {
+    "SEL": (BF, 2048), "GG": (BF, 2048), "ON1": (BF, 2048),
+    "ID": (BF, 128), "IDN": (BF, 128), "I1K": (BF, 128), "INK": (BF, 128), "I8K": (BF, 128), "I2K": (BF, 128), "IH": (BF, 128), "IHN": (BF, 128),
+    "BK": (BF, 128), "BKN": (BF, 128), "B32": (BF, 128), "BNK": (BF, 128), "B3K": (BF, 128), "BKC": (BF, 128),
+    "RST0": (BF, L), "RSTB": (BF, L), "RSTN": (BF, NC * C), "AK": (BF, 2 * NC * C), "SM": (BF, 2 * NC * C), "PCN": (H, 96), "TBC": (H, 96), "MC": (H, 96), "Z0": (BF, 192),
+    "RSTM": (BF, NC * C), "PRF": (H, 192), "CH": (F4, 8),
+    "IA": (I4, 96), "IB": (I4, 96), "IC": (I4, 96), "R6": (I4, 16), "C6": (I4, 16), "CM": (I4, 96),
+    "CL": (F4, 16), "C2": (F4, 16), "THR": (I4, 8), "NTH": (F4, 8), "NLIM": (F4, 8), "ACN": (F4, 8), "AS": (F4, 8), "AI": (I4, 8), "AI2": (I4, 8),
+    "VI": (I4, 24), "VI2": (I4, 24), "OFV": (U2, 24), "OFW": (U2, 16), "VL": (H, 16), "KB": (F4, 16), "WN": (F4, 16), "WN2": (F4, 16), "DV": (F4, 16), "WO": (F4, 16), "WO2": (F4, 16),
+    "SI": (I4, 1024), "SA": (F4, 1024), "SE": (H, 512), "SG": (H, 512), "SNE": (H, 512),
+}
+WHERE = {}
+_tot = {}
+for _n, (_d, _w) in [(n + str(h), x) for n, x in PER.items() for h in (0, 1)] + list(ONE.items()):
+    WHERE[_n] = (_d, _tot.get(_d, 0), _w)
+    _tot[_d] = _tot.get(_d, 0) + (_w + 15) // 16 * 16
+
+SCRATCH = {"p_" + _d: ("sbuf", [128, _w], _d) for _d, _w in _tot.items()}
+SCRATCH["tab"] = ("sbuf", [128, 4112], BF)
+for _n in ("scw", "stw", "sow"):
+    SCRATCH[_n] = ("sbuf", [128, 608], F4)
+for _h in (0, 1):
+    for _t in range(4):
+        SCRATCH["m%d%d" % (_t, _h)] = ("sbuf", [128, 288], H)
+        if _t < 3:
+            SCRATCH["o%d%d" % (_t, _h)] = ("sbuf", [128, 288], H)
+for _b in ("cm0", "cm1", "cm2", "pk", "pc", "ph", "px", "pm"):
+    SCRATCH[_b] = ("psum", [128, 512], F4)
+NLOAD, NOUT = 10, 7
+SEMAPHORES = ["v", "s", "t", "g", "loc"] + ["l%d" % i for i in range(NLOAD)] + ["a%d%d" % (t, h) for t in (1, 2, 3) for h in (0, 1)] + ["out%d" % i for i in range(NOUT)]
+
+K = {"v": 1.0e-3, "t": 0.5e-3, "fix": 0.06, "wake": 0.08, "gat": 1.56, "hop": 3.5}
+OTHER = [{}, {"gat": 1.1, "wake": 0.04}, {"gat": 2.0}, {"wake": 0.2, "hop": 5.0}, {"t": 0.75e-3}]
+TRIES = 250
+def cv(n, k=1.0): return K["fix"] + K["v"] * max(64, n * k)
+def ct(*ns): return sum(K["t"] * max(64, n) for n in ns) + 0.03
+
+MODES = ["SV", "SV", "SV", "SV", "SV", "SS"]
+NENG = 8
+PLAN = {}
+
+
+def build(T):
+    ops = []
+    now = [0]
+
+    def B(name, lo=0, hi=None, step=1):
+        d, a, w = WHERE[name]
+        hi = w if hi is None else hi
+        t = T["p_" + d]
+        return t[:, a + lo:a + hi] if step == 1 else t[:, a + lo:a + hi:step]
+
+    def op(eng, rd, wr, cost, fn, banks=(), lat=0.0, sem=None, val=1, get=None, put=None):
+        ops.append(dict(h=now[0], e=eng, r=rd.split(), w=wr.split(), c=cost, f=fn, lat=lat, sem=sem, val=val, b=list(banks), i=len(ops), get=get, put=put))
+
+    def mm(calls):
+        def f(q):
+            x = None
+            for o, a, b, s, e in (calls if isinstance(calls, list) else calls()):
+                x = q.matmul(o, a, b, s, e)
+            return x
+        return f
+
+    def group(out, pairs):
+        k = len(pairs)
+        return [(out if o is None else o, a, b, j == 0, j == k - 1) for j, (a, b, o) in enumerate(pairs)]
+
+    pool = lambda k: T["cm%d" % PLAN["bank"][k]]
+    sel = lambda l, nm="SEL": B(nm, 128 * l, 128 * l + 128)
+    V, S, TE, G, Y = "v", "s", "t", "g", "y"
+
+    def ts(rd, wr, out, i, s1, s2, o0, o1=None, n=96, k=1.0, banks=()):
+        op(V, rd, wr, cv(n, k), (lambda q: q.tensor_scalar(out, i, s1, s2, o0, o1)) if o1 is not None else (lambda q: q.tensor_scalar(out, i, s1, None, o0)), banks)
+    def tt(rd, wr, out, a, b, o, n=96, k=2.0, banks=()):
+        op(V, rd, wr, cv(n, k), lambda q: q.tensor_tensor(out, a, b, o), banks)
+    def cp(rd, wr, out, i, n=96, k=1.0, banks=()):
+        op(V, rd, wr, cv(n, k), lambda q: q.tensor_copy(out, i), banks)
+    def scan(rd, wr, out, a, b, o0, o1, n=96, k=1.0, banks=()):
+        op(V, rd, wr, cv(n, k), lambda q: q.tensor_tensor_scan(out, a, b, 0.0, o0, o1), banks)
+    def act(rd, wr, out, i, f, n=96, banks=(), k=1.0, **kw):
+        op(S, rd, wr, cv(n, k), lambda q: q.activation(out, i, f, **kw), banks)
+    def pe(rd, wr, calls, bank, *ns):
+        op(TE, rd, wr, ct(*ns), mm(calls), [bank])
+
+    def load(i, dst, out, src, eng=Y, rd="", kb=100):
+        op(eng, rd, dst, 0.1, lambda q: q.dma_start(out, src), lat=2.0 + kb / 250.0, sem="l%d" % i, val=16)
+    for h in (0, 1):
+        s = slice(C * h, C * h + C)
+        load(2 * h, "LIt%d" % h, B("LI%d" % h, 96, 192), T.tl[:, s], kb=50)
+        load(2 * h + 1, "LId%d" % h, B("LI%d" % h, 0, 96), T.dl[:, s], kb=50)
+        if h == 0:
+            load(4, "Z0", B("Z0"), T.z0[:], kb=50, eng=S)
+            op(V, "", "tabm", cv(8), lambda q: q.memset(T.tab[:, 2048:2056], -1.0))
+            load(5, "taba", T.tab[:, 0:2048], T.clk[:, 0:2048], kb=520)
+            load(6, "tabb", T.tab[:, 2049:4097], T.clk[:, 2048:4096], rd="tabm", eng=S, kb=520)
+    load(7, "SIc", B("SI", 0, 512), T.sc[:], kb=260)
+    load(8, "SIt", B("SI", 512, 1024), T.st[:], kb=260)
+    load(9, "THR", B("THR", 0, 1), T.th[:], kb=1)
+    TAB = "taba tabb tabm"
+    tab = T.tab[:, 0:4097]
+
+    def ms(name, c):
+        op(V, "", name, cv(WHERE[name][2], 0.5), lambda q: q.memset(B(name), c))
+    def iota(name, n, pat, base, cmul):
+        op(G, "", name, 0.13 + 2 * K["v"] * n, lambda q: q.iota(B(name, 0, n), pat, base, cmul))
+    def aff(out, src, n, pat, cmp, base, cmul):
+        op(G, src, out, 0.17 + 2 * K["v"] * n, lambda q: q.affine_select(B(out, 0, n), B(src, 0, n), pat, cmp, 0.0, base, cmul))
+    ms("ON1", 1.0)
+    aff("BKC", "ON1", 128, [[-16, 8], [0, 16]], A.is_ge, 0, 1)
+    aff("BK", "BKC", 128, [[16, 8], [0, 16]], A.is_ge, 15, -1)
+    aff("ID", "ON1", 128, [[-1, 128]], A.is_equal, 0, 1)
+    iota("IB", 96, [[0, 6], [-1, 16]], 15, 0)
+    aff("RST0", "ON1", L, [[0, C], [1, 16]], A.is_gt, 0, 0)
+    aff("SEL", "ON1", 2048, [[-1, 16], [-16, 8], [0, 16]], A.is_equal, 0, 1)
+    iota("IA", 96, [[0, 96]], 0, 1)
+    iota("CM", 96, [[1, 96]], 0, 0)
+    iota("C6", 12, [[0, 2], [16, 6]], 0, 0)
+    aff("RSTM", "ON1", NC * C, [[0, NC], [1, C]], A.is_equal, 0, 0)
+    ms("ZSS0", 0.0)
+    ms("ZSS1", 0.0)
+    act("RST0", "RSTB", B("RSTB"), B("RST0"), F.Copy, n=L, scale=2 * BIG, bias=-BIG)
+    act("RSTM", "RSTN", B("RSTN"), B("RSTM"), F.Copy, n=NC * C, scale=BIG)
+    act("ON1", "GG", B("GG"), B("ON1"), F.Copy, n=2048, scale=0.0)
+    for p in range(16):
+        act("BK GG", "GGp%d" % p, B("GG", 129 * p, 128 * p + 128, 16), B("BK", 0, 128, 16), F.Copy, n=8)
+    GGK = " ".join("GGp%d" % p for p in range(16))
+    for out, src, k in (("IDN", "ID", -1), ("I8K", "ID", 8192), ("BKN", "BK", -1), ("BNK", "BK", -1000), ("I1K", "ID", 1000), ("INK", "ID", -1000),
+                        ("B32", "BK", -1 / 32), ("B3K", "BK", 32), ("I2K", "ID", 2048), ("IH", "ID", 0.5), ("IHN", "ID", -0.5)):
+        act(src, out, B(out), B(src), F.Copy, n=128, scale=float(k))
+    ts("IB", "TBC", B("TBC"), B("IB"), 1 / 16, None, A.mult)
+    ts("IA", "IC", B("IC"), B("IA"), 15, None, A.bitwise_and)
+    ts("IC", "PCN", B("PCN"), B("IC"), -15.0, 1 / 16, A.add, A.mult)
+    ts("CM", "MC", B("MC"), B("CM"), 1 / 256, None, A.mult)
+    tt("C6 IC", "R6", B("R6", 0, 12), B("C6", 0, 12), B("IC", 0, 12), A.add, n=8)
+    ts("R6", "CL", B("CL", 0, 12), B("R6", 0, 12), 1 / 256, 512 + 48 / 256, A.mult, A.add, n=8)
+    ts("R6", "C2", B("C2", 0, 12), B("R6", 0, 12), 512.0, None, A.add, n=8)
+    ms("AS", 0.0)
+    ms("CH", -2048.0)
+    ts("THR", "NTH", B("NTH", 0, 1), B("THR", 0, 1), -1.0, -8192.0, A.mult, A.add, n=1)
+    cp("NTH", "NLIM0", B("NLIM", 0, 1), B("NTH", 0, 1), n=1)
+
+    def encode(out, ok, src, sk, tmp, tk, pa, ka, ba, pb, kb, bb, n):
+        ts(sk, ka, pa, src, 2048.0, -2048.0, A.is_ge, A.add, n=n, banks=[ba])
+        tt(sk + " " + ka, tk, tmp, pa, src, A.add, n=n, k=1, banks=[ba])
+        ts(sk, kb, pb, src, 0.0, None, A.is_ge, n=n, banks=[bb])
+        tt(tk + " " + kb, ok, out, pb, tmp, A.mult, n=n, k=1, banks=[bb])
+    for h in (0, 1):
+        m = T["m0%d" % h]
+        encode(m[:, 0:192], "m0%d" % h, B("LI%d" % h), "LIt%d LId%d" % (h, h), B("T1%d" % h), "T1%d" % h, T.pm[:, 0:192], "KC", "pm", T.pm[:, 192:384], "MK", "pm", 192)
+        act("Z0", "m0%dz" % h, m[:, 192:288], B("Z0", C * h, C * h + C), F.Copy)
+    encode(T.scw[:, 0:512], "scw", B("SI", 0, 512), "SIc", B("SA", 0, 512), "SAc", T.px[:], "px", "px", T.ph[:], "psH0 psH1 psV", "ph", 512)
+    encode(T.stw[:, 0:512], "stw", B("SI", 512, 1024), "SIt", B("SA", 512, 1024), "SAt", T.px[:], "px", "px", T.ph[:], "psH0 psH1 psV", "ph", 512)
+    op(V, "", "scwd", cv(96), lambda q: q.memset(T.scw[:, 512:608], 0.0))
+
+    def decode(out, ok, e, ek, sg, gk, ne, nk, n):
+        act(ek, gk, sg, e, F.Sign, n=n)
+        ts(ek, nk, ne, e, 0.0, None, A.not_equal, n=n, k=.5)
+        op(TE, "ID I2K IH IHN %s %s %s" % (ek, gk, nk), "dec" + gk, ct(n, n, n, n), mm(lambda: group(pool(gk)[:, 0:n], [
+            (B("ID"), e, None), (B("I2K"), ne, None), (B("IH"), ne, None), (B("IHN"), sg, None)])), get=gk)
+        op(S, "dec" + gk, ok, cv(n), lambda q: q.activation(out, pool(gk)[:, 0:n], F.Identity, bias=-1.0), put=gk)
+
+    nblk = [0]
+    def chunk(t, h):
+        now[0] = h
+        m = T["m%d%d" % (t, h)]
+        X = lambda n: n + str(h)
+        b = lambda n, *a: B(X(n), *a)
+        D, TT, Z = m[:, 0:96], m[:, 96:192], m[:, 192:288]
+        km = "m%d%d" % (t, h)
+        kz = km + "z" if t == 0 else km
+        x = lambda s: " ".join(X(w[1:]) if w[0] == "." else w for w in s.split())
+        pk, pc, ph, px, pm = T.pk, T.pc, T.ph, T.px, T.pm
+        cv0, cu0 = (96, 0) if h == 0 else (0, 96)
+        vo, uo = (6, 0) if h == 0 else (12, 18)
+        pv, pu, p0 = 192 + vo, 192 + uo, 192 + 12 * h
+        ts(km, x(".OFF"), b("OFF"), m[:, 0:192], 2048.0, None, A.add, n=192, k=.5)
+        cp(x(kz + " .ZSS"), x(".ZSS"), b("ZSS", 0, L, 16), Z, k=.5)
+        scan(x(".ZSS RST0"), x(".ZE"), b("ZE"), B("RST0"), b("ZSS"), A.mult, A.add, n=L, k=.5)
+        tt(x(TAB + " .OFF .ZE"), x(".MT"), b("MT"), tab.indirect(b("OFF", 96, 192)), b("ZE"), A.min, n=L, k=K["gat"])
+        pe(x(GGK + " ID ON1 .ZSS"), "psU%d" % h, group(pk[:, pu:pu + 6], [(B("ID"), B("ON1", 0, 6), None)] + [(sel(r, "GG"), b("ZSS", 16 * r, L, 256), None) for r in range(16)]), "pk", *[64] * 17)
+        pe(x(GGK + " ID TBC .MT"), "psK", group(pk[:, 0:96], [(B("ID"), B("TBC"), None)] + [(sel(r, "GG"), b("MT", 96 * r, 96 * r + 96), None) for r in range(16)]), "pk", *[96] * 17)
+        tt(x(TAB + " .OFF .ZE"), x(".SD"), b("SD"), tab.indirect(b("OFF", 0, 96)), b("ZE"), A.subtract, n=L, k=K["gat"])
+        act(x(".SD"), x(".AD"), b("AD"), b("SD"), F.Abs, n=L)
+        ts(km, x(".FL"), b("FL"), m[:, 0:192], 0.0, None, A.not_equal, n=192, k=.5)
+        pe(x("BK .FL"), "psA", group(pk[:, 256:352], [(B("BK"), b("FL", 96, 192), None)]), "pk", 96)
+        act("psA", x(".NH"), b("NH"), pk[:, 256:352], F.Relu, banks=["pk"], bias=2.0, scale=-2.0)
+        scan("psK RSTB", x(".MX"), b("MX"), B("RSTB", 0, 96), pk[:, 0:96], A.min, A.max, banks=["pk"])
+        ts(x(".MX"), x(".KI"), b("KI", 0, 6), b("MX", 15, 96, 16), -15 / 32, None, A.add, n=6)
+        tt(x(".MX .KI"), x(".QL"), b("QL", 0, 6), b("MX", 15, 96, 16), b("KI", 0, 6), A.subtract, n=6)
+        pe(x("SEL ID PCN .QL"), "psQ", group(None, [(B("ID"), B("PCN"), pk[:, 96:192])] + [(sel(r), b("QL", 0, 6), pk[:, 96 + 6 * r:102 + 6 * r]) for r in range(16)]), "pk", 96, *[64] * 16)
+        ts("psQ", x(".OH"), b("OH"), pk[:, 96:192], 0.0, None, A.is_equal, banks=["pk"])
+        tt(x(".OH " + km), x(".TH"), b("TH"), b("OH"), TT, A.mult)
+        pe(x(GGK + " .TH"), "psN%d" % h, group(pk[:, pv:pv + 6], [(sel(r, "GG"), b("TH", r, 96, 16), None) for r in range(16)]), "pk", *[64] * 16)
+        ts("psN%d psU%d" % (h, h), x(".VI"), B("VI", 12 * h, 12 * h + 12), pk[:, p0:p0 + 12], 1 - 2.0 ** -13, -0.5, A.mult, A.add, n=12, banks=["pk"])
+        ts(x(".VI"), x(".VI2"), B("VI2", 12 * h, 12 * h + 12), B("VI", 12 * h, 12 * h + 12), 511, None, A.bitwise_and, n=12)
+        cp(x(".VI2"), x(".OFV"), B("OFV", 12 * h, 12 * h + 12), B("VI2", 12 * h, 12 * h + 12), n=12)
+        ts("psN%d" % h, x(".OFN"), b("OFN", 0, 6), pk[:, pv:pv + 6], 2048.0, None, A.add, n=6, banks=["pk"])
+        act(x("scw scwd .OFV"), x(".CS"), b("CS"), T.scw[:, 0:512].indirect(B("OFV", 12 * h, 12 * h + 12)), F.Copy, n=192, k=K["gat"])
+        act(x("stw .OFV"), x(".CT"), b("CT"), T.stw[:, 0:512].indirect(B("OFV", 12 * h, 12 * h + 12)), F.Copy, n=192, k=K["gat"])
+        act(x(TAB + " .OFN"), x(".YK"), b("YK"), tab.indirect(b("OFN", 0, 6)), F.Copy, k=K["gat"])
+        def compare(j, src, ks, row, kr):
+            for k in range(4):
+                mode = MODES[2 * j + k // 2]
+                bank = "blk%d" % nblk[0]
+                nblk[0] += 1
+                op(TE, x("SEL IDN %s %s" % (ks, kr)), bank, ct(*[96] * 8), mm((lambda bank, k: lambda: [c for i in range(4) for c in group(
+                    pool(bank)[:, 96 * i:96 * i + 96], [(sel(4 * k + i), src, None), (B("IDN"), row, None)])])(bank, k)), get=bank)
+                a0 = 384 * k
+                eq, cx = b("EQ%d" % j, a0, a0 + 384), b("CX", L * j + a0, L * j + a0 + 384)
+                ke, kx = x(".EQ%d_%d_" % (j, k)), x(".CX%d_%d_" % (j, k))
+                if mode == "V":
+                    op(V, bank, ke, cv(384), (lambda bank, eq: lambda q: q.tensor_scalar(eq, pool(bank)[:, 0:384], 0.0, None, A.is_equal))(bank, eq), put=bank)
+                    continue
+                op(S, bank, kx, cv(384), (lambda bank, cx: lambda q: q.activation(cx, pool(bank)[:, 0:384], F.Abs))(bank, cx), put=bank)
+                if mode == "SS":
+                    act(kx, ke, eq, cx, F.Relu, n=384, bias=1.0, scale=-1.0)
+                elif k % 2:
+                    k0, a0 = k - 1, a0 - 384
+                    ts(kx + " " + x(".CX%d_%d_" % (j, k0)), ke + " " + x(".EQ%d_%d_" % (j, k0)), b("EQ%d" % j, a0, a0 + 768), b("CX", L * j + a0, L * j + a0 + 768), 0.0, None, A.is_equal, n=768, k=.5)
+        eqk = lambda j: " ".join(x(".EQ%d_%d_" % (j, k)) for k in range(4))
+        eqb = lambda j, l: b("EQ%d" % j, 96 * l, 96 * l + 96)
+        compare(0, D, km, TT, km)
+        pe(x(GGK + " ID %s .OH" % eqk(0)), "psC", group(pc[:, 0:96], [(sel(l, "GG"), eqb(0, l), None) for l in range(16)]) +
+           group(pc[:, 96:192], [(B("ID"), eqb(0, l), None) for l in range(16)] + [(B("ID"), b("OH"), None)]), "pc", *[96] * 33)
+        pe(x(GGK + " I8K .AD .FL"), "psD", group(pc[:, 192:288], [(B("I8K"), b("FL", 0, 96), None)] + [(sel(p, "GG"), b("AD", p, L, 16), None) for p in range(16)]), "pc", *[96] * 17)
+        act("psD NLIM%d" % t, x(".F1"), b("F1"), pc[:, 192:288], F.Relu, banks=["pc"], bias=B("NLIM", t, t + 1))
+        act("psC", "KC", pm[:, 0:192], pc[:, 0:192], F.Relu, n=192, banks=["pc", "pm"], bias=1.0, scale=-1.0)
+        tt("KC " + km, x(".DT1"), b("DT1"), pm[:, 0:192], m[:, 0:192], A.mult, n=192, k=1, banks=["pm"])
+        ts(x(".DT1"), x(".OFX"), b("OFX"), b("DT1", 0, 96), 2048.0, None, A.add, k=.5)
+        act(x(TAB + " .OFX"), x(".XT"), b("XT"), tab.indirect(b("OFX")), F.Copy, n=L, k=K["gat"])
+        tt(x("psC .F1"), x(".FAR"), b("FAR"), pc[:, 0:96], b("F1"), A.mult, k=1, banks=["pc"])
+        ts(x(".DT1"), x(".FD1"), b("FD1"), b("DT1"), 0.0, None, A.not_equal, n=192, k=.5)
+        scan(x(".XT RSTB"), x(".TP"), b("TP"), B("RSTB"), b("XT"), A.min, A.max, n=L, k=.5)
+        compare(1, D, km, b("CS", cv0, cv0 + 96), x(".CS"))
+        compare(2, TT, km, b("CT", cv0, cv0 + 96), x(".CT"))
+        for j in (0, 1):
+            pe("ID " + eqk(1 + j), "psH%d" % j, group(ph[:, 96 * j:96 * j + 96], [(B("ID"), eqb(1 + j, l), None) for l in range(16)]), "ph", *[96] * 16)
+        act("psH0 psH1", x(".HC"), b("HC"), ph[:, 0:192], F.Copy, n=192, banks=["ph"], bias=1 / 64)
+        far, left, nh = b("FAR"), b("FD1", 0, 96), b("NH")
+        calls = group(px[:, 192:288], [(B("ID"), B("ON1", 0, 96), None), (B("BKN"), left, None), (B("BNK"), far, None), (B("I1K"), nh, None)])
+        calls += group(px[:, 288:384], [(B("BK"), left, None), (B("BNK"), far, None), (B("INK"), nh, None)])
+        calls += group(px[:, 384:480], [(B("BK"), far, None)])
+        pe(x("ID ON1 BK BKN BNK I1K INK .FAR .FD1 .NH"), "px", calls, "px", *[96] * 8)
+        act("px CH", "MK", pm[:, 192:480], px[:, 192:480], F.Sigmoid, n=288, banks=["px", "pm"], bias=B("CH", 0, 1), scale=4096.0)
+        tt(x("MK .NH"), x(".PRF"), B("PRF", 96 * h, 96 * h + 96), pm[:, 192:288], nh, A.is_gt, k=1, banks=["pm"])
+        calls = [(px[:, 0:192], B("ID"), b("HC"), True, False), (px[:, 0:192], B("ID"), b("FD1"), False, False)]
+        for j in (0, 1):
+            for i, (w, y) in enumerate(((B("B32"), left), (B("BNK"), far), (B("I1K"), nh))):
+                calls.append((px[:, 96 * j:96 * j + 96], w, y, False, j == 1 and i == 2))
+        pe(x("ID B32 BNK I1K .HC .FD1 .FAR .NH"), "pxx px", calls, "px", 192, 192, *[96] * 6)
+        act("pxx", "KC", pm[:, 0:192], px[:, 0:192], F.Sigmoid, n=192, banks=["px", "pm"], scale=-16384.0)
+        for j, ck in ((0, ".CS"), (1, ".CT")):
+            s0, s1 = 96 * j, 96 * j + 96
+            tt(x("MK .DT1"), x(".P2%s_" % j), b("P2", s0, s1), pm[:, 288:384], b("DT1", s0, s1), A.mult, k=1, banks=["pm"])
+            tt(x("MK " + ck), x(".P3%s_" % j), b("P3", s0, s1), pm[:, 192:288], b(ck[1:], cu0, cu0 + 96), A.mult, k=1, banks=["pm"])
+            tt(x("KC " + ck), x(".P1%s_" % j), b("P1", s0, s1), pm[:, s0:s1], b(ck[1:], cv0, cv0 + 96), A.mult, k=1, banks=["pm"])
+        pe(x("ID IDN %s .YK" % kz), "psZ", group(pc[:, 384:480], [(B("ID"), Z, None), (B("IDN"), b("YK"), None)]), "pc", 96, 96)
+        act("psZ", x(".ZA"), b("ZA"), pc[:, 384:480], F.Abs, banks=["pc"])
+        pe(x("ID .YK .TP"), "psG", group(pk[:, 352:448], [(B("ID"), b("YK"), None), (B("ID"), b("TP", 15, L, 16), None)]), "pk", 96, 96)
+        act("psG", x(".ZG"), b("ZG"), pk[:, 352:448], F.Copy, banks=["pk"], bias=1023.75, scale=0.5)
+        act(x(".ZG"), x(".ZGI"), b("ZGI"), b("ZG"), F.Copy, bias=-1024.0)
+        tt(x("MK .ZA"), x(".ZA2"), b("ZA2"), pm[:, 384:480], b("ZA"), A.mult, k=1, banks=["pm"])
+        tt(x("MK .ZGI"), x(".ZG2"), b("ZG2"), pm[:, 288:384], b("ZGI"), A.mult, k=1, banks=["pm"])
+        tt(x("MK " + kz), x(".ZR"), b("ZR"), pm[:, 192:288], Z, A.mult, k=1, banks=["pm"])
+        calls = group(px[:, 0:192], [(B("ID"), b("P2"), None), (B("ID"), b("P3"), None), (B("ID"), b("P1"), None)])
+        calls += group(px[:, 192:288], [(B("ID"), b("ZA2"), None), (B("ID"), b("ZR"), None), (B("ID"), b("ZG2"), None)])
+        pe(x("ID .P10_ .P11_ .P20_ .P21_ .P30_ .P31_ .ZA2 .ZG2 .ZR"), "px pxx", calls, "px", 192, 192, 192, 96, 96, 96)
+        if t < 3:
+            ko = "o%d%d" % (t, h)
+            act("px", ko, T[ko][:], px[:, 0:288], F.Copy, n=288, banks=["px"])
+            op(G, ko, "m%d%d" % (t + 1, h), 1.0, ("send", t, h), lat=K["hop"], sem="a%d%d" % (t + 1, h), val=NENG)
+        else:
+            act("px", x(".FIN"), b("FIN"), px[:, 0:288], F.Copy, n=288, banks=["px"])
+            decode(b("OUT", 0, 192), x(".OUTa"), b("FIN", 0, 192), x(".FIN"), b("FSG"), x(".FSG"), b("FNE"), x(".FNE"), 192)
+            cp(x(".FIN"), x(".OUTz"), b("OUT", 192, 288), b("FIN", 192, 288))
+            s = slice(C * h, C * h + C)
+            for j, (y, k, a) in enumerate(((T.yd, ".OUTa", 0), (T.yt, ".OUTa", 96), (T.yz, ".OUTz", 192))):
+                op(Y, x(k), "y%d%d" % (j, h), 0.1, (lambda y, a: lambda q: q.dma_start(y[:, s], b("OUT", a, a + 96)))(y, a), lat=2.2, sem="out%d" % (3 * h + j), val=16)
+            decode(b("TD"), x(".TD"), b("DT1", 96, 192), x(".DT1"), b("TSG"), x(".TSG"), b("TNE"), x(".TNE"), 96)
+        if t < 3:
+            pe(x("BK BKN BNK .FL .FD1 .FAR"), "psS", group(pc[:, 288:384], [(B("BK"), b("FL", 0, 96), None), (B("BKN"), left, None), (B("BNK"), far, None)]), "pc", 96, 96, 96)
+            act("psS", x(".JK ACN%d%d" % (t, h)), b("JK"), pc[:, 288:384], F.Relu, banks=["pc"], accum_out=B("ACN", 2 * t + h, 2 * t + h + 1))
+
+    def proofs(t):
+        now[0] = 0
+        ph, n = T.ph, 12
+        w = lambda nm: B(nm, 0, 12)
+        v = B("VI2", 6, 18)
+        cp("VI20 VI21", "VL", w("VL"), v, n=n)
+        tt("VI20 VI21 CL", "KB", w("KB"), v, w("CL"), A.add, n=n)
+        tt("VI20 VI21 C2", "DV", w("DV"), v, w("C2"), A.subtract, n=n)
+        for h in (0, 1):
+            pe("ID MC SEL B3K VL PRF%d" % h, "psV", group(None, [(B("ID"), B("MC"), ph[:, 192:288])] + [(sel(r), B("VL", 6 * h, 6 * h + 6), ph[:, 192 + r:288:16]) for r in range(16)] +
+               [(B("B3K"), B("PRF", 96 * h, 96 * h + 96), ph[:, 192:288])]), "ph", 96, 96, *[64] * 16)
+            for c in range(NC):
+                a = 96 * (NC * h + c)
+                act("psV KB", "AK%d%d" % (h, c), B("AK", a, a + 96), ph[:, 192:288], F.Abs, banks=["ph"], bias=B("KB", 6 * h + c, 6 * h + c + 1), scale=-1.0)
+            a0, a1 = NC * C * h, NC * C * h + NC * C
+            scan("RSTN " + " ".join("AK%d%d" % (h, c) for c in range(NC)), "SM%d" % h, B("SM", a0, a1), B("RSTN"), B("AK", a0, a1), A.max, A.min, n=NC * C, k=.5)
+        pe(GGK + " PRF0 PRF1", "psP", group(ph[:, 384:396], [(sel(r, "GG"), B("PRF", r, 192, 16), None) for r in range(16)]), "ph", *[64] * 16)
+        ts("SM0 SM1", "WN", w("WN"), B("SM", 95, 2 * NC * C, 96), 47.5 / 256, 1 / 16, A.is_ge, A.mult, n=n)
+        tt("psP WN", "WN2", w("WN2"), ph[:, 384:396], w("WN"), A.mult, n=n, banks=["ph"])
+        tt("WN2 DV", "WO", w("WO"), w("WN2"), w("DV"), A.mult, n=n)
+        tt("WO C2", "WO2", w("WO2"), w("WO"), w("C2"), A.add, n=n)
+        cp("WO2", "OFW", w("OFW"), w("WO2"), n=n)
+        for h in (0, 1):
+            o = B("OFW", 6 * h, 6 * h + 6)
+            if t < 3:
+                cp("OFW DT1%d" % h, "scw scwd", T.scw[:, 0:608].indirect(o), B("DT1%d" % h, 96, 192), k=3)
+            else:
+                cp("OFW TD%d" % h, "sow", T.sow[:, 0:608].indirect(o), B("TD%d" % h), k=3)
+
+    for t in range(4):
+        if t == 3:
+            cp("scw", "SE", B("SE"), T.scw[:, 0:512], n=512)
+            op(V, "", "sowd", cv(96), lambda q: q.memset(T.sow[:, 512:608], 0.0))
+            decode(T.sow[:, 0:512], "sow", B("SE"), "SE", B("SG"), "SG", B("SNE"), "SNE", 512)
+            ops[-1]["r"].append("sowd")
+        for h in (0, 1):
+            chunk(t, h)
+        now[0] = 0
+        if t < 3:
+            op(V, "AS ACN%d0 ACN%d1" % (t, t), "AS", cv(1), (lambda t: lambda q: q.tensor_scalar(B("AS", t + 1, t + 2), B("ACN", 2 * t, 2 * t + 1), B("ACN", 2 * t + 1, 2 * t + 2), B("AS", t, t + 1), A.add, A.add))(t))
+            cp("AS", "AI", B("AI", 0, 1), B("AS", t + 1, t + 2), n=1)
+            ts("AI", "AI2", B("AI2", 0, 1), B("AI", 0, 1), 31, None, A.bitwise_and, n=1)
+            ts("AI2 NTH", "NLIM%d" % (t + 1), B("NLIM", t + 1, t + 2), B("AI2", 0, 1), -8.0, B("NTH", 0, 1), A.mult, A.add, n=1)
+        proofs(t)
+    op(Y, "sow", "ysd", 0.1, lambda q: q.dma_start(T.ys[:], T.sow[:, 0:512]), lat=2.5, sem="out6", val=16)
+    return ops
+
+
+def depend(ops):
+    last, readers = {}, {}
+    for o in ops:
+        o["d"] = {last[k] for k in o["r"] + o["w"] if k in last} | {i for k in o["w"] for i in readers.get(k, ())}
+        for k in o["r"]:
+            readers.setdefault(k, []).append(o["i"])
+        for k in o["w"]:
+            last[k] = o["i"]
+            readers[k] = []
+        o["d"].discard(o["i"])
+    return ops
+
+
+def schedule(ops, bend=None, rng=None):
+    n, wake = len(ops), K["wake"]
+    deps = [set(o["d"]) for o in ops]
+    succ = [[] for _ in ops]
+    left = [0] * n
+    for o in ops:
+        for i in o["d"]:
+            succ[i].append(o["i"]); left[o["i"]] += 1
+    pri = [0.0] * n
+    for o in reversed(ops):
+        pri[o["i"]] = o["c"] + o["lat"] + max([pri[j] + wake for j in succ[o["i"]]] or [0.0])
+    if bend:
+        noise = rng.normal(0.0, 1.0, n)
+        for o in ops: pri[o["i"]] += bend[0] * o["h"] + bend[1] * noise[o["i"]]
+    free, bank, end, base, order = {}, {}, [0.0] * n, {}, []
+    banks, given = [[0.0, None] for _ in range(3)], {}
+    ready = [o["i"] for o in ops if not left[o["i"]]]
+    def est(i):
+        o = ops[i]
+        x = max(free.get(o["e"], 0.0), base.get(i, 0.0))
+        for k in o["b"]:
+            e, tm = bank.get(k, ("", 0.0))
+            if e != o["e"]: x = max(x, tm + wake)
+        if o["get"]: x = max(x, min(p[0] for p in banks) + wake)
+        return x
+    while ready:
+        ests = [(est(i), i) for i in ready]
+        t0 = min(ests)[0]
+        best = None
+        for x, i in ests:
+            if x <= t0 + 0.02 and (best is None or pri[i] > pri[best[1]]): best = (x, i)
+        x, i = best
+        o = ops[i]
+        ready.remove(i)
+        free[o["e"]] = x + o["c"]
+        end[i] = x + o["c"] + o["lat"]
+        for k in o["b"]: bank[k] = (o["e"], x + o["c"])
+        if o["get"]:
+            j = min(range(3), key=lambda j: banks[j][0])
+            if banks[j][1] is not None: deps[i].add(banks[j][1])
+            given[o["get"]] = j
+            banks[j][0] = 1e9
+        if o["put"]: banks[given[o["put"]]] = [x + o["c"], i]
+        order.append(i)
+        for j in succ[i]:
+            base[j] = max(base.get(j, 0.0), end[i] + wake)
+            left[j] -= 1
+            if not left[j]: ready.append(j)
+    prev = {}
+    for i in order:
+        o = ops[i]
+        for k in o["b"]:
+            p = prev.setdefault(k, {})
+            for e, j in p.items():
+                if e != o["e"]: deps[i].add(j)
+            p[o["e"]] = i
+    return order, max(end), given, deps
+
+
+def lasts(ops, order, deps, costs, lats, wake):
+    free, end, t1 = {}, [0.0] * len(ops), 0.0
+    for i in order:
+        e = ops[i]["e"]
+        x = free.get(e, 0.0)
+        for j in deps[i]:
+            y = end[j] + wake
+            if y > x: x = y
+        free[e] = x + costs[i]
+        end[i] = y = x + costs[i] + lats[i]
+        if y > t1: t1 = y
+    return t1
+
+
+def plan(T):
+    models, k0 = [], dict(K)
+    for v in OTHER:
+        K.update(k0); K.update(v)
+        o = build(T)
+        models.append(([x["c"] for x in o], [x["lat"] for x in o], K["wake"]))
+    K.update(k0)
+    ops = depend(build(T))
+    rng = np.random.default_rng(1)
+    best = None
+    for k in range(TRIES):
+        bend = (0.0, 0.0) if k == 0 else (float(rng.uniform(-6, 1)), (0.0, 0.4, 0.8, 1.5)[k % 4])
+        order, tm, given, deps = schedule(ops, bend, rng)
+        score = sum(lasts(ops, order, deps, *x) for x in models)
+        if best is None or score < best[0]: best = (score, order, given, deps)
+    PLAN["score"], PLAN["order"], PLAN["bank"], PLAN["d"] = best
+
+
+def rank_program(g, core, T, topo):
+    rank = T.rank_of(core)
+    if rank is None:
+        return
+    if "order" not in PLAN:
+        plan(T)
+    ops = build(T)
+    queue = {"v": g.vector, "s": g.scalar, "t": g.tensor, "g": g, "y": g.sync}
+    know = {e: {} for e in queue}
+    count, clock = {}, {}
+    sends = 0
+    for i in PLAN["order"]:
+        o = ops[i]
+        e, q = o["e"], queue[o["e"]]
+        kn = know[e]
+        for j in sorted(PLAN["d"][i], key=lambda j: -clock[j][2]):
+            s, v, _, c = clock[j]
+            if kn.get(s, 0) < v:
+                q.wait_ge(T.sem[s], v)
+                for k, w in c.items():
+                    if kn.get(k, 0) < w: kn[k] = w
+                kn[s] = max(kn.get(s, 0), v)
+        if isinstance(o["f"], tuple):
+            _, t, h = o["f"]
+            dst = T.cores[(rank + HOPS[t]) % N]
+            rid, pid, _ = topo.addr(dst)
+            mask = sum(1 << x for x in topo.engines(core, dst)[:NENG])
+            g.remote_dma(T["m%d%d" % (t + 1, h)][:], T["o%d%d" % (t, h)][:], T.sem[o["sem"]], T.sem.loc, pid, rid, mask)
+            sends += NENG
+            clock[i] = (o["sem"], o["val"], len(clock), dict(kn))
+            continue
+        x = o["f"](q)
+        if o["sem"]:
+            x.then_inc(T.sem[o["sem"]], o["val"])
+            clock[i] = (o["sem"], o["val"], len(clock), dict(kn))
+        else:
+            count[e] = count.get(e, 0) + 1
+            x.then_inc(T.sem[e], 1)
+            clock[i] = (e, count[e], len(clock), dict(kn))
+    for e, c in count.items():
+        g.wait_ge(T.sem[e], c)
+    for i in range(NLOAD):
+        g.wait_ge(T.sem["l%d" % i], 16)
+    for i in range(NOUT):
+        g.wait_ge(T.sem["out%d" % i], 16)
+    g.wait_ge(T.sem.loc, sends)
+    for t in (1, 2, 3):
+        for h in (0, 1):
+            g.wait_ge(T.sem["a%d%d" % (t, h)], NENG)

@@ -17,7 +17,7 @@ PER = {
     "DT1": (H, 192), "FD1": (H, 192), "HC": (H, 192), "P1": (H, 192), "P2": (H, 192), "P3": (H, 192),
     "ZA": (H, 96), "ZA2": (H, 96), "ZG": (H, 96), "ZGI": (H, 96), "ZG2": (H, 96), "ZR": (H, 96),
     "FIN": (H, 288), "FSG": (H, 192), "FNE": (H, 192), "TSG": (H, 96), "TNE": (H, 96),
-    "MX": (F4, 96), "JK": (F4, 96), "T1": (F4, 192), "OUT": (F4, 288), "TD": (F4, 96),
+    "MX": (F4, 96), "JK": (F4, 96), "T1": (I4, 192), "OUT": (F4, 288), "TD": (F4, 96),
 }
 ONE = {
     "SEL": (BF, 2048), "GG": (BF, 2048), "ON1": (BF, 2048),
@@ -28,7 +28,7 @@ ONE = {
     "IA": (I4, 96), "IB": (I4, 96), "IC": (I4, 96), "R6": (I4, 16), "C6": (I4, 16), "CM": (I4, 96),
     "CL": (F4, 16), "C2": (F4, 16), "THR": (I4, 8), "NTH": (F4, 8), "NLIM": (F4, 8), "ACN": (F4, 8), "AS": (F4, 8), "AI": (I4, 8), "AI2": (I4, 8),
     "VI": (I4, 24), "VI2": (I4, 24), "OFV": (U2, 24), "OFW": (U2, 16), "VL": (H, 16), "KB": (F4, 16), "WN": (F4, 16), "WN2": (F4, 16), "DV": (F4, 16), "WO": (F4, 16), "WO2": (F4, 16),
-    "SI": (I4, 1024), "SA": (F4, 1024), "SE": (H, 512), "SG": (H, 512), "SNE": (H, 512),
+    "SI": (I4, 1024), "SA": (I4, 1024), "SE": (H, 512), "SG": (H, 512), "SNE": (H, 512),
 }
 WHERE = {}
 _tot = {}
@@ -51,8 +51,10 @@ NLOAD, NOUT = 10, 7
 SEMAPHORES = ["v", "s", "t", "g", "loc"] + ["l%d" % i for i in range(NLOAD)] + ["a%d%d" % (t, h) for t in (1, 2, 3) for h in (0, 1)] + ["out%d" % i for i in range(NOUT)]
 
 K = {"v": 1.0e-3, "t": 0.5e-3, "fix": 0.06, "wake": 0.08, "gat": 1.56, "hop": 3.5}
-OTHER = [{}, {"gat": 1.1, "wake": 0.04}, {"gat": 2.0}, {"wake": 0.2, "hop": 5.0}, {"t": 0.75e-3}]
-TRIES = 250
+SHIFTS = [5006, 5008, 5010, 5013, 5017, 5019, 5035, 5038, 5042, 5063, 5066, 5075, 5094, 5123, 5134, 5148, 5158, 5187, 5195, 5231, 5237, 5239, 6032, 6046, 6070, 6071, 6085,
+          6120, 6123, 6137, 6150, 6168, 6174, 6184, 6186, 6210, 6227, 16018, 16022, 16053, 16073, 16078, 16083, 16115, 16117, 16202, 16229, 16235, 25045, 25064, 25090, 25179,
+          25225, 25247, 25289, 25321, 25341, 31031, 31038, 31054, 31071, 31148, 31193, 31212, 31214, 31231, 31273, 31323, 36017, 36080, 36087, 36089, 36159, 36209, 36242, 36297,
+          36305, 46081, 46129, 46160, 46232]
 def cv(n, k=1.0): return K["fix"] + K["v"] * max(64, n * k)
 def ct(*ns): return sum(K["t"] * max(64, n) for n in ns) + 0.03
 
@@ -99,7 +101,7 @@ def build(T):
     def scan(rd, wr, out, a, b, o0, o1, n=96, k=1.0, banks=()):
         op(V, rd, wr, cv(n, k), lambda q: q.tensor_tensor_scan(out, a, b, 0.0, o0, o1), banks)
     def act(rd, wr, out, i, f, n=96, banks=(), k=1.0, **kw):
-        op(S, rd, wr, cv(n, k), lambda q: q.activation(out, i, f, **kw), banks)
+        op(S, rd, wr, K["fix"] + K["v"] * n * k, lambda q: q.activation(out, i, f, **kw), banks)
     def pe(rd, wr, calls, bank, *ns):
         op(TE, rd, wr, ct(*ns), mm(calls), [bank])
 
@@ -157,20 +159,20 @@ def build(T):
     ts("R6", "C2", B("C2", 0, 12), B("R6", 0, 12), 512.0, None, A.add, n=8)
     ms("AS", 0.0)
     ms("CH", -2048.0)
+    op(V, "", " ".join("AK%d%d" % (h, c) for h in (0, 1) for c in range(NC)), cv(2 * NC * C, 0.5), lambda q: q.memset(B("AK"), 512.0))
     ts("THR", "NTH", B("NTH", 0, 1), B("THR", 0, 1), -1.0, -8192.0, A.mult, A.add, n=1)
     cp("NTH", "NLIM0", B("NLIM", 0, 1), B("NTH", 0, 1), n=1)
 
-    def encode(out, ok, src, sk, tmp, tk, pa, ka, ba, pb, kb, bb, n):
-        ts(sk, ka, pa, src, 2048.0, -2048.0, A.is_ge, A.add, n=n, banks=[ba])
-        tt(sk + " " + ka, tk, tmp, pa, src, A.add, n=n, k=1, banks=[ba])
+    def encode(out, ok, src, sk, tmp, tk, pb, kb, bb, n):
+        ts(sk, tk, tmp, src, 1 + 2.0 ** -12, 2.0 ** -13 - 2048, A.mult, A.add, n=n)
         ts(sk, kb, pb, src, 0.0, None, A.is_ge, n=n, banks=[bb])
         tt(tk + " " + kb, ok, out, pb, tmp, A.mult, n=n, k=1, banks=[bb])
     for h in (0, 1):
         m = T["m0%d" % h]
-        encode(m[:, 0:192], "m0%d" % h, B("LI%d" % h), "LIt%d LId%d" % (h, h), B("T1%d" % h), "T1%d" % h, T.pm[:, 0:192], "KC", "pm", T.pm[:, 192:384], "MK", "pm", 192)
+        encode(m[:, 0:192], "m0%d" % h, B("LI%d" % h), "LIt%d LId%d" % (h, h), B("T1%d" % h), "T1%d" % h, T.pm[:, 192 * h:192 * h + 192], "KC MK", "pm", 192)
         act("Z0", "m0%dz" % h, m[:, 192:288], B("Z0", C * h, C * h + C), F.Copy)
-    encode(T.scw[:, 0:512], "scw", B("SI", 0, 512), "SIc", B("SA", 0, 512), "SAc", T.px[:], "px", "px", T.ph[:], "psH0 psH1 psV", "ph", 512)
-    encode(T.stw[:, 0:512], "stw", B("SI", 512, 1024), "SIt", B("SA", 512, 1024), "SAt", T.px[:], "px", "px", T.ph[:], "psH0 psH1 psV", "ph", 512)
+    encode(T.scw[:, 0:512], "scw", B("SI", 0, 512), "SIc", B("SA", 0, 512), "SAc", T.px[:], "px", "px", 512)
+    encode(T.stw[:, 0:512], "stw", B("SI", 512, 1024), "SIt", B("SA", 512, 1024), "SAt", T.ph[:], "psH0 psH1 psV", "ph", 512)
     op(V, "", "scwd", cv(96), lambda q: q.memset(T.scw[:, 512:608], 0.0))
 
     def decode(out, ok, e, ek, sg, gk, ne, nk, n):
@@ -315,7 +317,7 @@ def build(T):
                [(B("B3K"), B("PRF", 96 * h, 96 * h + 96), ph[:, 192:288])]), "ph", 96, 96, *[64] * 16)
             for c in range(NC):
                 a = 96 * (NC * h + c)
-                act("psV KB", "AK%d%d" % (h, c), B("AK", a, a + 96), ph[:, 192:288], F.Abs, banks=["ph"], bias=B("KB", 6 * h + c, 6 * h + c + 1), scale=-1.0)
+                act("psV KB", "AK%d%d" % (h, c), B("AK", a + 16 * c, a + 96), ph[:, 192 + 16 * c:288], F.Abs, n=96 - 16 * c, banks=["ph"], bias=B("KB", 6 * h + c, 6 * h + c + 1), scale=-1.0)
             a0, a1 = NC * C * h, NC * C * h + NC * C
             scan("RSTN " + " ".join("AK%d%d" % (h, c) for c in range(NC)), "SM%d" % h, B("SM", a0, a1), B("RSTN"), B("AK", a0, a1), A.max, A.min, n=NC * C, k=.5)
         pe(GGK + " PRF0 PRF1", "psP", group(ph[:, 384:396], [(sel(r, "GG"), B("PRF", r, 192, 16), None) for r in range(16)]), "ph", *[64] * 16)
@@ -363,7 +365,23 @@ def depend(ops):
     return ops
 
 
-def schedule(ops, bend=None, rng=None):
+def shifts(ops):
+    off = [-3.0 * o["h"] for o in ops]
+    kind = [(o["e"] + o["w"][0].rstrip("0123456789_"), o["h"]) for o in ops]
+    names = sorted(set(kind))
+    for i in SHIFTS:
+        rng = np.random.default_rng(i)
+        u, a, w, d = rng.random(), int(rng.integers(1 << 30)), int(rng.integers(4)), float(rng.normal())
+        if u < .5:
+            which, size = [j for j, k in enumerate(kind) if k == names[a % len(names)]], 3
+        else:
+            a %= len(ops)
+            which, size = range(a, min(len(ops), a + (1, 5, 20, 60)[w])), 4
+        for j in which: off[j] += size * d
+    return off
+
+
+def schedule(ops, off):
     n, wake = len(ops), K["wake"]
     deps = [set(o["d"]) for o in ops]
     succ = [[] for _ in ops]
@@ -374,9 +392,7 @@ def schedule(ops, bend=None, rng=None):
     pri = [0.0] * n
     for o in reversed(ops):
         pri[o["i"]] = o["c"] + o["lat"] + max([pri[j] + wake for j in succ[o["i"]]] or [0.0])
-    if bend:
-        noise = rng.normal(0.0, 1.0, n)
-        for o in ops: pri[o["i"]] += bend[0] * o["h"] + bend[1] * noise[o["i"]]
+    pri = [a + b for a, b in zip(pri, off)]
     free, bank, end, base, order = {}, {}, [0.0] * n, {}, []
     banks, given = [[0.0, None] for _ in range(3)], {}
     ready = [o["i"] for o in ops if not left[o["i"]]]
@@ -422,45 +438,14 @@ def schedule(ops, bend=None, rng=None):
     return order, max(end), given, deps
 
 
-def lasts(ops, order, deps, costs, lats, wake):
-    free, end, t1 = {}, [0.0] * len(ops), 0.0
-    for i in order:
-        e = ops[i]["e"]
-        x = free.get(e, 0.0)
-        for j in deps[i]:
-            y = end[j] + wake
-            if y > x: x = y
-        free[e] = x + costs[i]
-        end[i] = y = x + costs[i] + lats[i]
-        if y > t1: t1 = y
-    return t1
-
-
-def plan(T):
-    models, k0 = [], dict(K)
-    for v in OTHER:
-        K.update(k0); K.update(v)
-        o = build(T)
-        models.append(([x["c"] for x in o], [x["lat"] for x in o], K["wake"]))
-    K.update(k0)
-    ops = depend(build(T))
-    rng = np.random.default_rng(1)
-    best = None
-    for k in range(TRIES):
-        bend = (0.0, 0.0) if k == 0 else (float(rng.uniform(-6, 1)), (0.0, 0.4, 0.8, 1.5)[k % 4])
-        order, tm, given, deps = schedule(ops, bend, rng)
-        score = sum(lasts(ops, order, deps, *x) for x in models)
-        if best is None or score < best[0]: best = (score, order, given, deps)
-    PLAN["score"], PLAN["order"], PLAN["bank"], PLAN["d"] = best
-
-
 def rank_program(g, core, T, topo):
     rank = T.rank_of(core)
     if rank is None:
         return
-    if "order" not in PLAN:
-        plan(T)
     ops = build(T)
+    if "order" not in PLAN:
+        depend(ops)
+        PLAN["order"], PLAN["time"], PLAN["bank"], PLAN["d"] = schedule(ops, shifts(ops))
     queue = {"v": g.vector, "s": g.scalar, "t": g.tensor, "g": g, "y": g.sync}
     know = {e: {} for e in queue}
     count, clock = {}, {}

import numpy as np
from concourse.mybir import dt, AluOpType as A, ActivationFunctionType as F

N = 6
HOPS = [1, 2, 3]
M, C, NC = 192, 96, 6
L = 16 * C
BIG = 30000.0

H, BF, F4, I4, U2 = "float16", "bfloat16", "float32", "int32", "uint16"
PER = {
    "OFF": (U2, 192), "OFX": (U2, 96), "OFN": (U2, 8), "LI": (I4, 192), "KI": (I4, 8),
    "ZSS": (BF, L), "ZE": (H, L), "MT": (H, L), "SD": (H, L), "AD": (H, L), "XT": (H, L), "TP": (H, L),
    "EQ0": (H, L), "EQ1": (H, L), "EQ2": (H, L), "CX": (H, 3 * L),
    "FL": (H, 192), "QL": (H, 8), "OH": (H, 96), "TH": (H, 96), "NH": (H, 96),
    "CS": (H, 192), "CT": (H, 192), "YK": (H, 96), "F1": (H, 96), "FAR": (H, 96),
    "DT1": (H, 192), "FD1": (H, 192), "HC": (H, 192), "P1": (H, 192), "P2": (H, 192), "P3": (H, 192),
    "ZA": (H, 96), "ZA2": (H, 96), "ZG": (H, 96), "ZGI": (H, 96), "ZG2": (H, 96), "ZR": (H, 96),
    "FIN": (H, 288), "FSG": (H, 192), "FNE": (H, 192), "TSG": (H, 96), "TNE": (H, 96),
    "MX": (F4, 96), "JK": (F4, 96), "T1": (I4, 192), "OUT": (F4, 288), "TD": (F4, 96),
}
ONE = {
    "SEL": (BF, 2048), "GG": (BF, 2048), "ON1": (BF, 2048),
    "ID": (BF, 128), "IDN": (BF, 128), "I1K": (BF, 128), "INK": (BF, 128), "I8K": (BF, 128), "I2K": (BF, 128), "IH": (BF, 128), "IHN": (BF, 128),
    "BK": (BF, 128), "BKN": (BF, 128), "B32": (BF, 128), "BNK": (BF, 128), "B3K": (BF, 128), "BKC": (BF, 128),
    "RST0": (BF, L), "RSTB": (BF, L), "RSTN": (BF, NC * C), "AK": (BF, 2 * NC * C), "SM": (BF, 2 * NC * C), "PCN": (H, 96), "TBC": (H, 96), "MC": (H, 96), "Z0": (BF, 192),
    "RSTM": (BF, NC * C), "PRF": (H, 192), "CH": (F4, 8),
    "IA": (I4, 96), "IB": (I4, 96), "IC": (I4, 96), "R6": (I4, 16), "C6": (I4, 16), "CM": (I4, 96),
    "CL": (F4, 16), "C2": (F4, 16), "THR": (I4, 8), "NTH": (F4, 8), "NLIM": (F4, 8), "ACN": (F4, 8), "AS": (F4, 8), "AI": (I4, 8), "AI2": (I4, 8),
    "VI": (I4, 24), "VI2": (I4, 24), "OFV": (U2, 24), "OFW": (U2, 16), "VL": (H, 16), "KB": (F4, 16), "WN": (F4, 16), "WN2": (F4, 16), "DV": (F4, 16), "WO": (F4, 16), "WO2": (F4, 16),
    "SI": (I4, 1024), "SA": (I4, 1024), "SE": (H, 512), "SG": (H, 512), "SNE": (H, 512),
}
WHERE = {}
_tot = {}
for _n, (_d, _w) in [(n + str(h), x) for n, x in PER.items() for h in (0, 1)] + list(ONE.items()):
    WHERE[_n] = (_d, _tot.get(_d, 0), _w)
    _tot[_d] = _tot.get(_d, 0) + (_w + 15) // 16 * 16

SCRATCH = {"p_" + _d: ("sbuf", [128, _w], _d) for _d, _w in _tot.items()}
SCRATCH["tab"] = ("sbuf", [128, 4112], BF)
for _n in ("scw", "stw", "sow"):
    SCRATCH[_n] = ("sbuf", [128, 608], F4)
for _h in (0, 1):
    for _t in range(4):
        SCRATCH["m%d%d" % (_t, _h)] = ("sbuf", [128, 288], H)
        if _t < 3:
            SCRATCH["o%d%d" % (_t, _h)] = ("sbuf", [128, 288], H)
for _b in ("cm0", "cm1", "cm2", "pk", "pc", "ph", "px", "pm"):
    SCRATCH[_b] = ("psum", [128, 512], F4)
NLOAD, NOUT = 10, 7
SEMAPHORES = ["v", "s", "t", "g", "loc"] + ["l%d" % i for i in range(NLOAD)] + ["a%d%d" % (t, h) for t in (1, 2, 3) for h in (0, 1)] + ["out%d" % i for i in range(NOUT)]

K = {"v": 1.0e-3, "t": 0.5e-3, "fix": 0.06, "wake": 0.08, "gat": 1.56, "hop": 3.5}
SHIFTS = [5006, 5008, 5010, 5013, 5017, 5019, 5035, 5038, 5042, 5063, 5066, 5075, 5094, 5123, 5134, 5148, 5158, 5187, 5195, 5231, 5237, 5239, 6032, 6046, 6070, 6071, 6085,
          6120, 6123, 6137, 6150, 6168, 6174, 6184, 6186, 6210, 6227, 16018, 16022, 16053, 16073, 16078, 16083, 16115, 16117, 16202, 16229, 16235, 25045, 25064, 25090, 25179,
          25225, 25247, 25289, 25321, 25341, 31031, 31038, 31054, 31071, 31148, 31193, 31212, 31214, 31231, 31273, 31323, 36017, 36080, 36087, 36089, 36159, 36209, 36242, 36297,
          36305, 46081, 46129, 46160, 46232]
def cv(n, k=1.0): return K["fix"] + K["v"] * max(64, n * k)
def ct(*ns): return sum(K["t"] * max(64, n) for n in ns) + 0.03

MODES = ["SV", "SV", "SV", "SV", "SV", "SS"]
NENG = 8
PLAN = {}


def build(T):
    ops = []
    now = [0]

    def B(name, lo=0, hi=None, step=1):
        d, a, w = WHERE[name]
        hi = w if hi is None else hi
        t = T["p_" + d]
        return t[:, a + lo:a + hi] if step == 1 else t[:, a + lo:a + hi:step]

    def op(eng, rd, wr, cost, fn, banks=(), lat=0.0, sem=None, val=1, get=None, put=None):
        ops.append(dict(h=now[0], e=eng, r=rd.split(), w=wr.split(), c=cost, f=fn, lat=lat, sem=sem, val=val, b=list(banks), i=len(ops), get=get, put=put))

    def mm(calls):
        def f(q):
            x = None
            for o, a, b, s, e in (calls if isinstance(calls, list) else calls()):
                x = q.matmul(o, a, b, s, e)
            return x
        return f

    def group(out, pairs):
        k = len(pairs)
        return [(out if o is None else o, a, b, j == 0, j == k - 1) for j, (a, b, o) in enumerate(pairs)]

    pool = lambda k: T["cm%d" % PLAN["bank"][k]]
    sel = lambda l, nm="SEL": B(nm, 128 * l, 128 * l + 128)
    V, S, TE, G, Y = "v", "s", "t", "g", "y"

    def ts(rd, wr, out, i, s1, s2, o0, o1=None, n=96, k=1.0, banks=()):
        op(V, rd, wr, cv(n, k), (lambda q: q.tensor_scalar(out, i, s1, s2, o0, o1)) if o1 is not None else (lambda q: q.tensor_scalar(out, i, s1, None, o0)), banks)
    def tt(rd, wr, out, a, b, o, n=96, k=2.0, banks=()):
        op(V, rd, wr, cv(n, k), lambda q: q.tensor_tensor(out, a, b, o), banks)
    def cp(rd, wr, out, i, n=96, k=1.0, banks=()):
        op(V, rd, wr, cv(n, k), lambda q: q.tensor_copy(out, i), banks)
    def scan(rd, wr, out, a, b, o0, o1, n=96, k=1.0, banks=()):
        op(V, rd, wr, cv(n, k), lambda q: q.tensor_tensor_scan(out, a, b, 0.0, o0, o1), banks)
    def act(rd, wr, out, i, f, n=96, banks=(), k=1.0, **kw):
        op(S, rd, wr, K["fix"] + K["v"] * n * k, lambda q: q.activation(out, i, f, **kw), banks)
    def pe(rd, wr, calls, bank, *ns):
        op(TE, rd, wr, ct(*ns), mm(calls), [bank])

    def load(i, dst, out, src, eng=Y, rd="", kb=100):
        op(eng, rd, dst, 0.1, lambda q: q.dma_start(out, src), lat=2.0 + kb / 250.0, sem="l%d" % i, val=16)
    for h in (0, 1):
        s = slice(C * h, C * h + C)
        load(2 * h, "LIt%d" % h, B("LI%d" % h, 96, 192), T.tl[:, s], kb=50)
        load(2 * h + 1, "LId%d" % h, B("LI%d" % h, 0, 96), T.dl[:, s], kb=50)
        if h == 0:
            load(4, "Z0", B("Z0"), T.z0[:], kb=50, eng=S)
            op(V, "", "tabm", cv(8), lambda q: q.memset(T.tab[:, 2048:2056], -1.0))
            load(5, "taba", T.tab[:, 0:2048], T.clk[:, 0:2048], kb=520)
            load(6, "tabb", T.tab[:, 2049:4097], T.clk[:, 2048:4096], rd="tabm", eng=S, kb=520)
    load(7, "SIc", B("SI", 0, 512), T.sc[:], kb=260)
    load(8, "SIt", B("SI", 512, 1024), T.st[:], kb=260)
    load(9, "THR", B("THR", 0, 1), T.th[:], kb=1)
    TAB = "taba tabb tabm"
    tab = T.tab[:, 0:4097]

    def ms(name, c):
        op(V, "", name, cv(WHERE[name][2], 0.5), lambda q: q.memset(B(name), c))
    def iota(name, n, pat, base, cmul):
        op(G, "", name, 0.13 + 2 * K["v"] * n, lambda q: q.iota(B(name, 0, n), pat, base, cmul))
    def aff(out, src, n, pat, cmp, base, cmul):
        op(G, src, out, 0.17 + 2 * K["v"] * n, lambda q: q.affine_select(B(out, 0, n), B(src, 0, n), pat, cmp, 0.0, base, cmul))
    ms("ON1", 1.0)
    aff("BKC", "ON1", 128, [[-16, 8], [0, 16]], A.is_ge, 0, 1)
    aff("BK", "BKC", 128, [[16, 8], [0, 16]], A.is_ge, 15, -1)
    aff("ID", "ON1", 128, [[-1, 128]], A.is_equal, 0, 1)
    iota("IB", 96, [[0, 6], [-1, 16]], 15, 0)
    aff("RST0", "ON1", L, [[0, C], [1, 16]], A.is_gt, 0, 0)
    aff("SEL", "ON1", 2048, [[-1, 16], [-16, 8], [0, 16]], A.is_equal, 0, 1)
    iota("IA", 96, [[0, 96]], 0, 1)
    iota("CM", 96, [[1, 96]], 0, 0)
    iota("C6", 12, [[0, 2], [16, 6]], 0, 0)
    aff("RSTM", "ON1", NC * C, [[0, NC], [1, C]], A.is_equal, 0, 0)
    ms("ZSS0", 0.0)
    ms("ZSS1", 0.0)
    act("RST0", "RSTB", B("RSTB"), B("RST0"), F.Copy, n=L, scale=2 * BIG, bias=-BIG)
    act("RSTM", "RSTN", B("RSTN"), B("RSTM"), F.Copy, n=NC * C, scale=BIG)
    act("ON1", "GG", B("GG"), B("ON1"), F.Copy, n=2048, scale=0.0)
    for p in range(16):
        act("BK GG", "GGp%d" % p, B("GG", 129 * p, 128 * p + 128, 16), B("BK", 0, 128, 16), F.Copy, n=8)
    GGK = " ".join("GGp%d" % p for p in range(16))
    for out, src, k in (("IDN", "ID", -1), ("I8K", "ID", 8192), ("BKN", "BK", -1), ("BNK", "BK", -1000), ("I1K", "ID", 1000), ("INK", "ID", -1000),
                        ("B32", "BK", -1 / 32), ("B3K", "BK", 32), ("I2K", "ID", 2048), ("IH", "ID", 0.5), ("IHN", "ID", -0.5)):
        act(src, out, B(out), B(src), F.Copy, n=128, scale=float(k))
    ts("IB", "TBC", B("TBC"), B("IB"), 1 / 16, None, A.mult)
    ts("IA", "IC", B("IC"), B("IA"), 15, None, A.bitwise_and)
    ts("IC", "PCN", B("PCN"), B("IC"), -15.0, 1 / 16, A.add, A.mult)
    ts("CM", "MC", B("MC"), B("CM"), 1 / 256, None, A.mult)
    tt("C6 IC", "R6", B("R6", 0, 12), B("C6", 0, 12), B("IC", 0, 12), A.add, n=8)
    ts("R6", "CL", B("CL", 0, 12), B("R6", 0, 12), 1 / 256, 512 + 48 / 256, A.mult, A.add, n=8)
    ts("R6", "C2", B("C2", 0, 12), B("R6", 0, 12), 512.0, None, A.add, n=8)
    ms("AS", 0.0)
    ms("CH", -2048.0)
    op(V, "", " ".join("AK%d%d" % (h, c) for h in (0, 1) for c in range(NC)), cv(2 * NC * C, 0.5), lambda q: q.memset(B("AK"), 512.0))
    ts("THR", "NTH", B("NTH", 0, 1), B("THR", 0, 1), -1.0, -8192.0, A.mult, A.add, n=1)
    cp("NTH", "NLIM0", B("NLIM", 0, 1), B("NTH", 0, 1), n=1)

    def encode(out, ok, src, sk, tmp, tk, pb, kb, bb, n):
        ts(sk, tk, tmp, src, 1 + 2.0 ** -12, 2.0 ** -13 - 2048, A.mult, A.add, n=n)
        ts(sk, kb, pb, src, 0.0, None, A.is_ge, n=n, banks=[bb])
        tt(tk + " " + kb, ok, out, pb, tmp, A.mult, n=n, k=1, banks=[bb])
    for h in (0, 1):
        m = T["m0%d" % h]
        encode(m[:, 0:192], "m0%d" % h, B("LI%d" % h), "LIt%d LId%d" % (h, h), B("T1%d" % h), "T1%d" % h, T.pm[:, 192 * h:192 * h + 192], "KC MK", "pm", 192)
        act("Z0", "m0%dz" % h, m[:, 192:288], B("Z0", C * h, C * h + C), F.Copy)
    encode(T.scw[:, 0:512], "scw", B("SI", 0, 512), "SIc", B("SA", 0, 512), "SAc", T.px[:], "px", "px", 512)
    encode(T.stw[:, 0:512], "stw", B("SI", 512, 1024), "SIt", B("SA", 512, 1024), "SAt", T.ph[:], "psH0 psH1 psV", "ph", 512)
    op(V, "", "scwd", cv(96), lambda q: q.memset(T.scw[:, 512:608], 0.0))

    def decode(out, ok, e, ek, sg, gk, ne, nk, n):
        act(ek, gk, sg, e, F.Sign, n=n)
        ts(ek, nk, ne, e, 0.0, None, A.not_equal, n=n, k=.5)
        op(TE, "ID I2K IH IHN %s %s %s" % (ek, gk, nk), "dec" + gk, ct(n, n, n, n), mm(lambda: group(pool(gk)[:, 0:n], [
            (B("ID"), e, None), (B("I2K"), ne, None), (B("IH"), ne, None), (B("IHN"), sg, None)])), get=gk)
        op(S, "dec" + gk, ok, cv(n), lambda q: q.activation(out, pool(gk)[:, 0:n], F.Identity, bias=-1.0), put=gk)

    nblk = [0]
    def chunk(t, h):
        now[0] = h
        m = T["m%d%d" % (t, h)]
        X = lambda n: n + str(h)
        b = lambda n, *a: B(X(n), *a)
        D, TT, Z = m[:, 0:96], m[:, 96:192], m[:, 192:288]
        km = "m%d%d" % (t, h)
        kz = km + "z" if t == 0 else km
        x = lambda s: " ".join(X(w[1:]) if w[0] == "." else w for w in s.split())
        pk, pc, ph, px, pm = T.pk, T.pc, T.ph, T.px, T.pm
        cv0, cu0 = (96, 0) if h == 0 else (0, 96)
        vo, uo = (6, 0) if h == 0 else (12, 18)
        pv, pu, p0 = 192 + vo, 192 + uo, 192 + 12 * h
        ts(km, x(".OFF"), b("OFF"), m[:, 0:192], 2048.0, None, A.add, n=192, k=.5)
        cp(x(kz + " .ZSS"), x(".ZSS"), b("ZSS", 0, L, 16), Z, k=.5)
        scan(x(".ZSS RST0"), x(".ZE"), b("ZE"), B("RST0"), b("ZSS"), A.mult, A.add, n=L, k=.5)
        tt(x(TAB + " .OFF .ZE"), x(".MT"), b("MT"), tab.indirect(b("OFF", 96, 192)), b("ZE"), A.min, n=L, k=K["gat"])
        pe(x(GGK + " ID ON1 .ZSS"), "psU%d" % h, group(pk[:, pu:pu + 6], [(B("ID"), B("ON1", 0, 6), None)] + [(sel(r, "GG"), b("ZSS", 16 * r, L, 256), None) for r in range(16)]), "pk", *[64] * 17)
        pe(x(GGK + " ID TBC .MT"), "psK", group(pk[:, 0:96], [(B("ID"), B("TBC"), None)] + [(sel(r, "GG"), b("MT", 96 * r, 96 * r + 96), None) for r in range(16)]), "pk", *[96] * 17)
        tt(x(TAB + " .OFF .ZE"), x(".SD"), b("SD"), tab.indirect(b("OFF", 0, 96)), b("ZE"), A.subtract, n=L, k=K["gat"])
        act(x(".SD"), x(".AD"), b("AD"), b("SD"), F.Abs, n=L)
        ts(km, x(".FL"), b("FL"), m[:, 0:192], 0.0, None, A.not_equal, n=192, k=.5)
        pe(x("BK .FL"), "psA", group(pk[:, 256:352], [(B("BK"), b("FL", 96, 192), None)]), "pk", 96)
        act("psA", x(".NH"), b("NH"), pk[:, 256:352], F.Relu, banks=["pk"], bias=2.0, scale=-2.0)
        scan("psK RSTB", x(".MX"), b("MX"), B("RSTB", 0, 96), pk[:, 0:96], A.min, A.max, banks=["pk"])
        ts(x(".MX"), x(".KI"), b("KI", 0, 6), b("MX", 15, 96, 16), -15 / 32, None, A.add, n=6)
        tt(x(".MX .KI"), x(".QL"), b("QL", 0, 6), b("MX", 15, 96, 16), b("KI", 0, 6), A.subtract, n=6)
        pe(x("SEL ID PCN .QL"), "psQ", group(None, [(B("ID"), B("PCN"), pk[:, 96:192])] + [(sel(r), b("QL", 0, 6), pk[:, 96 + 6 * r:102 + 6 * r]) for r in range(16)]), "pk", 96, *[64] * 16)
        ts("psQ", x(".OH"), b("OH"), pk[:, 96:192], 0.0, None, A.is_equal, banks=["pk"])
        tt(x(".OH " + km), x(".TH"), b("TH"), b("OH"), TT, A.mult)
        pe(x(GGK + " .TH"), "psN%d" % h, group(pk[:, pv:pv + 6], [(sel(r, "GG"), b("TH", r, 96, 16), None) for r in range(16)]), "pk", *[64] * 16)
        ts("psN%d psU%d" % (h, h), x(".VI"), B("VI", 12 * h, 12 * h + 12), pk[:, p0:p0 + 12], 1 - 2.0 ** -13, -0.5, A.mult, A.add, n=12, banks=["pk"])
        ts(x(".VI"), x(".VI2"), B("VI2", 12 * h, 12 * h + 12), B("VI", 12 * h, 12 * h + 12), 511, None, A.bitwise_and, n=12)
        cp(x(".VI2"), x(".OFV"), B("OFV", 12 * h, 12 * h + 12), B("VI2", 12 * h, 12 * h + 12), n=12)
        ts("psN%d" % h, x(".OFN"), b("OFN", 0, 6), pk[:, pv:pv + 6], 2048.0, None, A.add, n=6, banks=["pk"])
        act(x("scw scwd .OFV"), x(".CS"), b("CS"), T.scw[:, 0:512].indirect(B("OFV", 12 * h, 12 * h + 12)), F.Copy, n=192, k=K["gat"])
        act(x("stw .OFV"), x(".CT"), b("CT"), T.stw[:, 0:512].indirect(B("OFV", 12 * h, 12 * h + 12)), F.Copy, n=192, k=K["gat"])
        act(x(TAB + " .OFN"), x(".YK"), b("YK"), tab.indirect(b("OFN", 0, 6)), F.Copy, k=K["gat"])
        def compare(j, src, ks, row, kr):
            for k in range(4):
                mode = MODES[2 * j + k // 2]
                bank = "blk%d" % nblk[0]
                nblk[0] += 1
                op(TE, x("SEL IDN %s %s" % (ks, kr)), bank, ct(*[96] * 8), mm((lambda bank, k: lambda: [c for i in range(4) for c in group(
                    pool(bank)[:, 96 * i:96 * i + 96], [(sel(4 * k + i), src, None), (B("IDN"), row, None)])])(bank, k)), get=bank)
                a0 = 384 * k
                eq, cx = b("EQ%d" % j, a0, a0 + 384), b("CX", L * j + a0, L * j + a0 + 384)
                ke, kx = x(".EQ%d_%d_" % (j, k)), x(".CX%d_%d_" % (j, k))
                if mode == "V":
                    op(V, bank, ke, cv(384), (lambda bank, eq: lambda q: q.tensor_scalar(eq, pool(bank)[:, 0:384], 0.0, None, A.is_equal))(bank, eq), put=bank)
                    continue
                op(S, bank, kx, cv(384), (lambda bank, cx: lambda q: q.activation(cx, pool(bank)[:, 0:384], F.Abs))(bank, cx), put=bank)
                if mode == "SS":
                    act(kx, ke, eq, cx, F.Relu, n=384, bias=1.0, scale=-1.0)
                elif k % 2:
                    k0, a0 = k - 1, a0 - 384
                    ts(kx + " " + x(".CX%d_%d_" % (j, k0)), ke + " " + x(".EQ%d_%d_" % (j, k0)), b("EQ%d" % j, a0, a0 + 768), b("CX", L * j + a0, L * j + a0 + 768), 0.0, None, A.is_equal, n=768, k=.5)
        eqk = lambda j: " ".join(x(".EQ%d_%d_" % (j, k)) for k in range(4))
        eqb = lambda j, l: b("EQ%d" % j, 96 * l, 96 * l + 96)
        compare(0, D, km, TT, km)
        pe(x(GGK + " ID %s .OH" % eqk(0)), "psC", group(pc[:, 0:96], [(sel(l, "GG"), eqb(0, l), None) for l in range(16)]) +
           group(pc[:, 96:192], [(B("ID"), eqb(0, l), None) for l in range(16)] + [(B("ID"), b("OH"), None)]), "pc", *[96] * 33)
        pe(x(GGK + " I8K .AD .FL"), "psD", group(pc[:, 192:288], [(B("I8K"), b("FL", 0, 96), None)] + [(sel(p, "GG"), b("AD", p, L, 16), None) for p in range(16)]), "pc", *[96] * 17)
        act("psD NLIM%d" % t, x(".F1"), b("F1"), pc[:, 192:288], F.Relu, banks=["pc"], bias=B("NLIM", t, t + 1))
        act("psC", "KC", pm[:, 0:192], pc[:, 0:192], F.Relu, n=192, banks=["pc", "pm"], bias=1.0, scale=-1.0)
        tt("KC " + km, x(".DT1"), b("DT1"), pm[:, 0:192], m[:, 0:192], A.mult, n=192, k=1, banks=["pm"])
        ts(x(".DT1"), x(".OFX"), b("OFX"), b("DT1", 0, 96), 2048.0, None, A.add, k=.5)
        act(x(TAB + " .OFX"), x(".XT"), b("XT"), tab.indirect(b("OFX")), F.Copy, n=L, k=K["gat"])
        tt(x("psC .F1"), x(".FAR"), b("FAR"), pc[:, 0:96], b("F1"), A.mult, k=1, banks=["pc"])
        ts(x(".DT1"), x(".FD1"), b("FD1"), b("DT1"), 0.0, None, A.not_equal, n=192, k=.5)
        scan(x(".XT RSTB"), x(".TP"), b("TP"), B("RSTB"), b("XT"), A.min, A.max, n=L, k=.5)
        compare(1, D, km, b("CS", cv0, cv0 + 96), x(".CS"))
        compare(2, TT, km, b("CT", cv0, cv0 + 96), x(".CT"))
        for j in (0, 1):
            pe("ID " + eqk(1 + j), "psH%d" % j, group(ph[:, 96 * j:96 * j + 96], [(B("ID"), eqb(1 + j, l), None) for l in range(16)]), "ph", *[96] * 16)
        act("psH0 psH1", x(".HC"), b("HC"), ph[:, 0:192], F.Copy, n=192, banks=["ph"], bias=1 / 64)
        far, left, nh = b("FAR"), b("FD1", 0, 96), b("NH")
        calls = group(px[:, 192:288], [(B("ID"), B("ON1", 0, 96), None), (B("BKN"), left, None), (B("BNK"), far, None), (B("I1K"), nh, None)])
        calls += group(px[:, 288:384], [(B("BK"), left, None), (B("BNK"), far, None), (B("INK"), nh, None)])
        calls += group(px[:, 384:480], [(B("BK"), far, None)])
        pe(x("ID ON1 BK BKN BNK I1K INK .FAR .FD1 .NH"), "px", calls, "px", *[96] * 8)
        act("px CH", "MK", pm[:, 192:480], px[:, 192:480], F.Sigmoid, n=288, banks=["px", "pm"], bias=B("CH", 0, 1), scale=4096.0)
        tt(x("MK .NH"), x(".PRF"), B("PRF", 96 * h, 96 * h + 96), pm[:, 192:288], nh, A.is_gt, k=1, banks=["pm"])
        calls = [(px[:, 0:192], B("ID"), b("HC"), True, False), (px[:, 0:192], B("ID"), b("FD1"), False, False)]
        for j in (0, 1):
            for i, (w, y) in enumerate(((B("B32"), left), (B("BNK"), far), (B("I1K"), nh))):
                calls.append((px[:, 96 * j:96 * j + 96], w, y, False, j == 1 and i == 2))
        pe(x("ID B32 BNK I1K .HC .FD1 .FAR .NH"), "pxx px", calls, "px", 192, 192, *[96] * 6)
        act("pxx", "KC", pm[:, 0:192], px[:, 0:192], F.Sigmoid, n=192, banks=["px", "pm"], scale=-16384.0)
        for j, ck in ((0, ".CS"), (1, ".CT")):
            s0, s1 = 96 * j, 96 * j + 96
            tt(x("MK .DT1"), x(".P2%s_" % j), b("P2", s0, s1), pm[:, 288:384], b("DT1", s0, s1), A.mult, k=1, banks=["pm"])
            tt(x("MK " + ck), x(".P3%s_" % j), b("P3", s0, s1), pm[:, 192:288], b(ck[1:], cu0, cu0 + 96), A.mult, k=1, banks=["pm"])
            tt(x("KC " + ck), x(".P1%s_" % j), b("P1", s0, s1), pm[:, s0:s1], b(ck[1:], cv0, cv0 + 96), A.mult, k=1, banks=["pm"])
        pe(x("ID IDN %s .YK" % kz), "psZ", group(pc[:, 384:480], [(B("ID"), Z, None), (B("IDN"), b("YK"), None)]), "pc", 96, 96)
        act("psZ", x(".ZA"), b("ZA"), pc[:, 384:480], F.Abs, banks=["pc"])
        pe(x("ID .YK .TP"), "psG", group(pk[:, 352:448], [(B("ID"), b("YK"), None), (B("ID"), b("TP", 15, L, 16), None)]), "pk", 96, 96)
        act("psG", x(".ZG"), b("ZG"), pk[:, 352:448], F.Copy, banks=["pk"], bias=1023.75, scale=0.5)
        act(x(".ZG"), x(".ZGI"), b("ZGI"), b("ZG"), F.Copy, bias=-1024.0)
        tt(x("MK .ZA"), x(".ZA2"), b("ZA2"), pm[:, 384:480], b("ZA"), A.mult, k=1, banks=["pm"])
        tt(x("MK .ZGI"), x(".ZG2"), b("ZG2"), pm[:, 288:384], b("ZGI"), A.mult, k=1, banks=["pm"])
        tt(x("MK " + kz), x(".ZR"), b("ZR"), pm[:, 192:288], Z, A.mult, k=1, banks=["pm"])
        calls = group(px[:, 0:192], [(B("ID"), b("P2"), None), (B("ID"), b("P3"), None), (B("ID"), b("P1"), None)])
        calls += group(px[:, 192:288], [(B("ID"), b("ZA2"), None), (B("ID"), b("ZR"), None), (B("ID"), b("ZG2"), None)])
        pe(x("ID .P10_ .P11_ .P20_ .P21_ .P30_ .P31_ .ZA2 .ZG2 .ZR"), "px pxx", calls, "px", 192, 192, 192, 96, 96, 96)
        if t < 3:
            ko = "o%d%d" % (t, h)
            act("px", ko, T[ko][:], px[:, 0:288], F.Copy, n=288, banks=["px"])
            op(G, ko, "m%d%d" % (t + 1, h), 1.0, ("send", t, h), lat=K["hop"], sem="a%d%d" % (t + 1, h), val=NENG)
        else:
            act("px", x(".FIN"), b("FIN"), px[:, 0:288], F.Copy, n=288, banks=["px"])
            decode(b("OUT", 0, 192), x(".OUTa"), b("FIN", 0, 192), x(".FIN"), b("FSG"), x(".FSG"), b("FNE"), x(".FNE"), 192)
            cp(x(".FIN"), x(".OUTz"), b("OUT", 192, 288), b("FIN", 192, 288))
            s = slice(C * h, C * h + C)
            for j, (y, k, a) in enumerate(((T.yd, ".OUTa", 0), (T.yt, ".OUTa", 96), (T.yz, ".OUTz", 192))):
                op(Y, x(k), "y%d%d" % (j, h), 0.1, (lambda y, a: lambda q: q.dma_start(y[:, s], b("OUT", a, a + 96)))(y, a), lat=2.2, sem="out%d" % (3 * h + j), val=16)
            decode(b("TD"), x(".TD"), b("DT1", 96, 192), x(".DT1"), b("TSG"), x(".TSG"), b("TNE"), x(".TNE"), 96)
        if t < 3:
            pe(x("BK BKN BNK .FL .FD1 .FAR"), "psS", group(pc[:, 288:384], [(B("BK"), b("FL", 0, 96), None), (B("BKN"), left, None), (B("BNK"), far, None)]), "pc", 96, 96, 96)
            act("psS", x(".JK ACN%d%d" % (t, h)), b("JK"), pc[:, 288:384], F.Relu, banks=["pc"], accum_out=B("ACN", 2 * t + h, 2 * t + h + 1))

    def proofs(t):
        now[0] = 0
        ph, n = T.ph, 12
        w = lambda nm: B(nm, 0, 12)
        v = B("VI2", 6, 18)
        cp("VI20 VI21", "VL", w("VL"), v, n=n)
        tt("VI20 VI21 CL", "KB", w("KB"), v, w("CL"), A.add, n=n)
        tt("VI20 VI21 C2", "DV", w("DV"), v, w("C2"), A.subtract, n=n)
        for h in (0, 1):
            pe("ID MC SEL B3K VL PRF%d" % h, "psV", group(None, [(B("ID"), B("MC"), ph[:, 192:288])] + [(sel(r), B("VL", 6 * h, 6 * h + 6), ph[:, 192 + r:288:16]) for r in range(16)] +
               [(B("B3K"), B("PRF", 96 * h, 96 * h + 96), ph[:, 192:288])]), "ph", 96, 96, *[64] * 16)
            for c in range(NC):
                a = 96 * (NC * h + c)
                act("psV KB", "AK%d%d" % (h, c), B("AK", a + 16 * c, a + 96), ph[:, 192 + 16 * c:288], F.Abs, n=96 - 16 * c, banks=["ph"], bias=B("KB", 6 * h + c, 6 * h + c + 1), scale=-1.0)
            a0, a1 = NC * C * h, NC * C * h + NC * C
            scan("RSTN " + " ".join("AK%d%d" % (h, c) for c in range(NC)), "SM%d" % h, B("SM", a0, a1), B("RSTN"), B("AK", a0, a1), A.max, A.min, n=NC * C, k=.5)
        pe(GGK + " PRF0 PRF1", "psP", group(ph[:, 384:396], [(sel(r, "GG"), B("PRF", r, 192, 16), None) for r in range(16)]), "ph", *[64] * 16)
        ts("SM0 SM1", "WN", w("WN"), B("SM", 95, 2 * NC * C, 96), 47.5 / 256, 1 / 16, A.is_ge, A.mult, n=n)
        tt("psP WN", "WN2", w("WN2"), ph[:, 384:396], w("WN"), A.mult, n=n, banks=["ph"])
        tt("WN2 DV", "WO", w("WO"), w("WN2"), w("DV"), A.mult, n=n)
        tt("WO C2", "WO2", w("WO2"), w("WO"), w("C2"), A.add, n=n)
        cp("WO2", "OFW", w("OFW"), w("WO2"), n=n)
        for h in (0, 1):
            o = B("OFW", 6 * h, 6 * h + 6)
            if t < 3:
                cp("OFW DT1%d" % h, "scw scwd", T.scw[:, 0:608].indirect(o), B("DT1%d" % h, 96, 192), k=3)
            else:
                cp("OFW TD%d" % h, "sow", T.sow[:, 0:608].indirect(o), B("TD%d" % h), k=3)

    for t in range(4):
        if t == 3:
            cp("scw", "SE", B("SE"), T.scw[:, 0:512], n=512)
            op(V, "", "sowd", cv(96), lambda q: q.memset(T.sow[:, 512:608], 0.0))
            decode(T.sow[:, 0:512], "sow", B("SE"), "SE", B("SG"), "SG", B("SNE"), "SNE", 512)
            ops[-1]["r"].append("sowd")
        for h in (0, 1):
            chunk(t, h)
        now[0] = 0
        if t < 3:
            op(V, "AS ACN%d0 ACN%d1" % (t, t), "AS", cv(1), (lambda t: lambda q: q.tensor_scalar(B("AS", t + 1, t + 2), B("ACN", 2 * t, 2 * t + 1), B("ACN", 2 * t + 1, 2 * t + 2), B("AS", t, t + 1), A.add, A.add))(t))
            cp("AS", "AI", B("AI", 0, 1), B("AS", t + 1, t + 2), n=1)
            ts("AI", "AI2", B("AI2", 0, 1), B("AI", 0, 1), 31, None, A.bitwise_and, n=1)
            ts("AI2 NTH", "NLIM%d" % (t + 1), B("NLIM", t + 1, t + 2), B("AI2", 0, 1), -8.0, B("NTH", 0, 1), A.mult, A.add, n=1)
        proofs(t)
    op(Y, "sow", "ysd", 0.1, lambda q: q.dma_start(T.ys[:], T.sow[:, 0:512]), lat=2.5, sem="out6", val=16)
    return ops


def depend(ops):
    last, readers = {}, {}
    for o in ops:
        o["d"] = {last[k] for k in o["r"] + o["w"] if k in last} | {i for k in o["w"] for i in readers.get(k, ())}
        for k in o["r"]:
            readers.setdefault(k, []).append(o["i"])
        for k in o["w"]:
            last[k] = o["i"]
            readers[k] = []
        o["d"].discard(o["i"])
    return ops


def shifts(ops):
    off = [-3.0 * o["h"] for o in ops]
    kind = [(o["e"] + o["w"][0].rstrip("0123456789_"), o["h"]) for o in ops]
    names = sorted(set(kind))
    for i in SHIFTS:
        rng = np.random.default_rng(i)
        u, a, w, d = rng.random(), int(rng.integers(1 << 30)), int(rng.integers(4)), float(rng.normal())
        if u < .5:
            which, size = [j for j, k in enumerate(kind) if k == names[a % len(names)]], 3
        else:
            a %= len(ops)
            which, size = range(a, min(len(ops), a + (1, 5, 20, 60)[w])), 4
        for j in which: off[j] += size * d
    return off


def schedule(ops, off):
    n, wake = len(ops), K["wake"]
    deps = [set(o["d"]) for o in ops]
    succ = [[] for _ in ops]
    left = [0] * n
    for o in ops:
        for i in o["d"]:
            succ[i].append(o["i"]); left[o["i"]] += 1
    pri = [0.0] * n
    for o in reversed(ops):
        pri[o["i"]] = o["c"] + o["lat"] + max([pri[j] + wake for j in succ[o["i"]]] or [0.0])
    pri = [a + b for a, b in zip(pri, off)]
    free, bank, end, base, order = {}, {}, [0.0] * n, {}, []
    banks, given = [[0.0, None] for _ in range(3)], {}
    ready = [o["i"] for o in ops if not left[o["i"]]]
    def est(i):
        o = ops[i]
        x = max(free.get(o["e"], 0.0), base.get(i, 0.0))
        for k in o["b"]:
            e, tm = bank.get(k, ("", 0.0))
            if e != o["e"]: x = max(x, tm + wake)
        if o["get"]: x = max(x, min(p[0] for p in banks) + wake)
        return x
    while ready:
        ests = [(est(i), i) for i in ready]
        t0 = min(ests)[0]
        best = None
        for x, i in ests:
            if x <= t0 + 0.02 and (best is None or pri[i] > pri[best[1]]): best = (x, i)
        x, i = best
        o = ops[i]
        ready.remove(i)
        free[o["e"]] = x + o["c"]
        end[i] = x + o["c"] + o["lat"]
        for k in o["b"]: bank[k] = (o["e"], x + o["c"])
        if o["get"]:
            j = min(range(3), key=lambda j: banks[j][0])
            if banks[j][1] is not None: deps[i].add(banks[j][1])
            given[o["get"]] = j
            banks[j][0] = 1e9
        if o["put"]: banks[given[o["put"]]] = [x + o["c"], i]
        order.append(i)
        for j in succ[i]:
            base[j] = max(base.get(j, 0.0), end[i] + wake)
            left[j] -= 1
            if not left[j]: ready.append(j)
    prev = {}
    for i in order:
        o = ops[i]
        for k in o["b"]:
            p = prev.setdefault(k, {})
            for e, j in p.items():
                if e != o["e"]: deps[i].add(j)
            p[o["e"]] = i
    return order, max(end), given, deps


def rank_program(g, core, T, topo):
    rank = T.rank_of(core)
    if rank is None:
        return
    ops = build(T)
    if "order" not in PLAN:
        depend(ops)
        PLAN["order"], PLAN["time"], PLAN["bank"], PLAN["d"] = schedule(ops, shifts(ops))
    queue = {"v": g.vector, "s": g.scalar, "t": g.tensor, "g": g, "y": g.sync}
    know = {e: {} for e in queue}
    count, clock = {}, {}
    sends = 0
    for i in PLAN["order"]:
        o = ops[i]
        e, q = o["e"], queue[o["e"]]
        kn = know[e]
        for j in sorted(PLAN["d"][i], key=lambda j: -clock[j][2]):
            s, v, _, c = clock[j]
            if kn.get(s, 0) < v:
                q.wait_ge(T.sem[s], v)
                for k, w in c.items():
                    if kn.get(k, 0) < w: kn[k] = w
                kn[s] = max(kn.get(s, 0), v)
        if isinstance(o["f"], tuple):
            _, t, h = o["f"]
            dst = T.cores[(rank + HOPS[t]) % N]
            rid, pid, _ = topo.addr(dst)
            mask = sum(1 << x for x in topo.engines(core, dst)[:NENG])
            g.remote_dma(T["m%d%d" % (t + 1, h)][:], T["o%d%d" % (t, h)][:], T.sem[o["sem"]], T.sem.loc, pid, rid, mask)
            sends += NENG
            clock[i] = (o["sem"], o["val"], len(clock), dict(kn))
            continue
        x = o["f"](q)
        if o["sem"]:
            x.then_inc(T.sem[o["sem"]], o["val"])
            clock[i] = (o["sem"], o["val"], len(clock), dict(kn))
        else:
            count[e] = count.get(e, 0) + 1
            x.then_inc(T.sem[e], 1)
            clock[i] = (e, count[e], len(clock), dict(kn))
    for e, c in count.items():
        g.wait_ge(T.sem[e], c)
    for i in range(NLOAD):
        g.wait_ge(T.sem["l%d" % i], 16)
    for i in range(NOUT):
        g.wait_ge(T.sem["out%d" % i], 16)
    g.wait_ge(T.sem.loc, sends)
    for t in (1, 2, 3):
        for h in (0, 1):
            g.wait_ge(T.sem["a%d%d" % (t, h)], NENG)
